import numpy as np, ml_dtypes
CORES = [51,54,179,182]
N = 4
BF = ml_dtypes.bfloat16
def gentries(a):
    return np.ascontiguousarray(a.reshape(8, 16, -1).transpose(0, 2, 1)).reshape(8, -1)
def gtable(e):
    e = np.asarray(e); return np.ascontiguousarray(e.reshape(8, -1, 16).transpose(0, 2, 1)).reshape(128, -1).astype(np.int32)
S, K, SH, AC, RO, Z = 1024, 2048, 1, 9, 4, 256
def one(w):
    c = np.add.accumulate(w, dtype=np.int64)
    return np.searchsorted(K * c, np.arange(K) * c[-1], side="right")
def ancestors(x, y, e):
    w = np.maximum(1, np.add.reduce(np.abs(x - y) <= e, axis=1, dtype=np.int64) >> SH)
    return np.stack([one(a) for a in w])
def parts(rng):
    fp = rng.random((N, 8, 16, S), dtype=np.float32); bp = rng.random((N, 8, 16, S), dtype=np.float32)
    nz = (rng.random((N, 8, 16, S), dtype=np.float32) - 0.5) * 0.125
    ob = 0.3 + 0.6 * rng.random((N, 8, 16, RO))
    lev = np.array([0.12, 0.18, 0.25, 0.36, 0.12, 0.18, 0.25, 0.36])[np.argsort(rng.random((N, 8)), axis=-1)][..., None]
    ep = lev * (0.7 + 0.6 * rng.random((N, 8, 16))); la = 0.2 + 0.6 * rng.random((N, 8, 16))
    r1 = 2.8 + 1.1 * rng.random((N, 8, 16)); r2 = 2.8 + 1.1 * rng.random((N, 8, 16))
    return fp, bp, nz, ob, ep, la, r1, r2, np.argsort(rng.random((N, 8, K)), axis=-1)
def pack(fp, bp, nz, ob, ep, la, r1, r2, p):
    d = {"f0": fp.reshape(N, 128, S).astype(BF), "b0": bp.reshape(N, 128, S).astype(BF), "nz": nz.reshape(N, 128, S).astype(BF), "obs": ob.reshape(N, 128, RO).astype(np.float32)}
    for k, v in (("eps", ep), ("lam", la), ("rf", r1), ("rb", r2)): d[k] = v.reshape(N, 128, 1).astype(np.float32)
    d["pi"] = np.stack([gtable(a) for a in p])
    return d
def pairing(rng, sf, sb, nand, n):
    h = max(1, AC >> SH)
    u = sf[one(np.where(sf != nand, h, 1))]; v = sb[one(np.where(sb != nand, h, 1))]
    a = rng.permutation(np.flatnonzero(u)); c = np.flatnonzero(~u); x = rng.permutation(np.flatnonzero(v)); z = rng.permutation(np.flatnonzero(~v))
    n = max(len(a) + len(x) - K, min(n, len(a), len(x))); p = np.zeros(K, np.int64)
    p[a[:n]] = x[:n]; p[a[n:]] = z[:len(a) - n]; p[c] = rng.permutation(np.concatenate([x[n:], z[len(a) - n:]]))
    return p
def setup_inputs(rng):
    return pack(*parts(rng))
def setup_inputs_spread(rng):
    fp, bp, nz, ob, ep, la, r1, r2, p = parts(rng); s = (N, 8, 1, S)
    fp = fp * np.exp2(-rng.integers(0, 4, s)) * (rng.random(s) > 0.0625); bp = bp * np.exp2(-rng.integers(0, 4, s)) * (rng.random(s) > 0.0625)
    nz = 2 * nz * np.exp2(-rng.integers(0, 4, s)) * (rng.random(s) > 0.0625)
    ob = 0.05 + 0.85 * rng.random(ob.shape); ep = np.exp2(-4 + 3 * rng.random((N, 8, 1))) * (0.7 + 0.3 * rng.random(ep.shape))
    la = rng.random(la.shape); r1 = 2 + 2 * rng.random(r1.shape); r2 = 2 + 2 * rng.random(r2.shape)
    return pack(fp, bp, nz, ob, ep, la, r1, r2, p)
def bits(rng, *s):
    return rng.integers(0, 2, s).astype(np.float32)
def setup_inputs_ends(rng):
    fp = bits(rng, N, 8, 16, S); bp = bits(rng, N, 8, 16, S); nz = 0.25 * bits(rng, N, 8, 16, S) - 0.125; ob = bits(rng, N, 8, 16, RO)
    cnt = rng.choice(np.array([7, 8, 9, 10]), (N, 8)); cnt[:, 0] = 0; cnt[:, 1] = 8; cnt[:, 2] = 9; cnt[:, 5] = 16; cnt[:, 7] = 16
    ep = (np.argsort(rng.random((N, 8, 16)), axis=-1) < cnt[..., None]).astype(np.float32)
    la = bits(rng, N, 8, 16); r1 = 4 * bits(rng, N, 8, 16); r2 = 4 * bits(rng, N, 8, 16)
    for x in (fp, bp):
        x[:, 0] = 1 - ob[:, 0, :, :1]
        for s in (0, S - 1): x[:, 0, :, s] = ob[:, 0, :, 0]
    mid = 1 + np.argsort(rng.random((N, 8, K - 2)), axis=-1); e = np.zeros((N, 8, 1), np.int64)
    p = np.concatenate([e + K - 1, mid, e], axis=2); p[:, 1::2] = p[:, 1::2, ::-1].copy()
    return pack(fp, bp, nz, ob, ep, la, r1, r2, p)
def crowd(rng):
    pools = []
    for turn in (0, 3):
        h = np.zeros((N, 8, S), np.int64)
        for q in range(N):
            for g in range(8):
                k = (g + q + turn) % 8
                if k == 0: h[q, g] = 16
                if k == 1: h[q, g] = 16; h[q, g, S - 1] = 15
                if k == 2: h[q, g] = rng.choice(np.array([0, 2 ** SH - 1, 2 ** SH, 15, 16]), S)
                if k == 3: h[q, g] = rng.integers(8, 10, S)
                if k == 4: h[q, g, 0] = 16
                if k == 6: h[q, g] = rng.integers(7, 10, S)
                if k == 7: h[q, g] = 16; h[q, g, 0] = 8
        order = np.argsort(rng.random((N, 8, 16, S), dtype=np.float32), axis=2)
        hit = rng.choice(np.array([0.375, 0.625], np.float32), (N, 8, 16, S)); miss = rng.choice(np.array([0.25, 0.75, 0.62890625], np.float32), (N, 8, 16, S))
        pools.append(np.where(order < h[:, :, None, :], hit, miss))
    return pools
def setup_inputs_corners(rng):
    fp, bp, nz, ob, ep, la, r1, r2, p = parts(rng); fp = 0.9 * fp; bp = 0.9 * bp; h = max(1, AC >> SH)
    for q in range(0, N, 2):
        for g in range(8):
            t = min(K, (0, 1, 2, K - 1, K, 2 * S - 1, 2 * S, 2 * S + 1)[(g + q) % 8]); nand = 4 * t > 3 * K; n = K - t if nand else t
            z = 3 * S // (2 * h + 3) if K <= 4 * t and not nand else S // (h + 2)
            sf = rng.permutation(S) < z; sb = rng.permutation(S) < z; m = rng.permutation(16) < AC
            fp[q, g, m] = np.where(sf, 0.625, 0.125); bp[q, g, m] = np.where(sb, 0.625, 0.125)
            ob[q, g, :, 0] = np.where(m, 0.125 if nand else 0.625, 1.0); ep[q, g] = np.where(m, 0.25 if nand else 0.125, 0.0); la[q, g] = np.where(m, 0.5, la[q, g])
            p[q, g] = pairing(rng, sf, sb, nand, n)
    cf, cb = crowd(rng)
    for q in range(1, N, 2):
        fp[q] = cf[q]; bp[q] = cb[q]; ob[q, :, :, 0] = 0.5; ep[q] = 0.125
        o = (q // 2) % 2; la[q, o::2] = 0.0; la[q, 1 - o::2] = 1.0
    return pack(fp, bp, nz, ob, ep, la, r1, r2, p)
def setup_inputs_calm(rng):
    fp, bp, nz, ob, ep, la, r1, r2, p = parts(rng); fp = 0.9 * fp; bp = 0.9 * bp; h = max(1, AC >> SH)
    r1 = 2.8 + 0.7 * rng.random(r1.shape); r2 = 2.8 + 0.7 * rng.random(r2.shape)
    m = rng.permutation(16) < AC; r1[..., m] = 0; r2[..., m] = 0
    zs = np.argsort(rng.random((N, 8, S)), axis=-1) < S // (h + 2)
    for q in range(N):
        for g in range(8):
            nand = (g // 4 + q) % 2 == 1; sf = zs[(q - 1) % N, g]; sb = zs[(q + 1) % N, (g - 1) % 8]
            nz[q, g, m] = np.where(zs[q, g], 0.125, -0.125 * rng.integers(0, 2, (AC, S)))
            fp[q, g, m] = np.where(sf, 0.125, 0.0); bp[q, g, m] = np.where(sb, 0.125, 0.0)
            ob[q, g] = np.where(m, 0.0 if nand else 0.125, 1.0)[:, None]; ep[q, g] = np.where(m, 0.0625 if nand else 0.03125, 0.0); la[q, g] = np.where(m, 0.5, la[q, g])
            p[q, g] = pairing(rng, sf, sb, nand, (g + q) % 4)
    return pack(fp, bp, nz, ob, ep, la, r1, r2, p)
def setup_inputs_rounding(rng):
    fp, bp, nz, ob, ep, la, r1, r2, p = parts(rng); ep[:] = 0.0; m = rng.permutation(16) < AC
    r1 = 2.8 + 0.7 * rng.random(r1.shape); r2 = 2.8 + 0.7 * rng.random(r2.shape); s = (N, 8, AC)
    kd = rng.permutation(np.array([0, 0, 0, 1, 1, 2, 2, 3]))[None, :, None]; none = np.float32(0)
    x, w, z = [a.astype(BF).astype(np.float32) for a in (0.1 + 0.8 * rng.random(s), 0.1 + 0.8 * rng.random(s), 0.125 * (rng.random(s) - 0.5))]
    x = np.where(kd == 3, none, x); z = np.where(kd == 3, none, z); la[:, :, m] = np.where(kd == 3, 0.0, la[:, :, m])
    e = (2.0 ** -6 + 2.0 ** -24 * rng.integers(1, 2 ** 18, s)).astype(np.float32)
    ep[:, :, m] = np.where(kd == 1, e, np.where(kd == 2, np.nextafter(e, none), none))
    fp[:, :, m] = x[..., None]; bp[:, :, m] = w[..., None]; nz[:, :, m] = z[..., None]
    j = rng.permutation(np.flatnonzero(~m))[:2]
    fp[:, :, j] = np.where(kd[..., None] < 2, np.float32(1), fp[:, :, j]); bp[:, :, j] = 0; nz[:, :, j] = 0
    la[:, :, j] = np.where(kd < 2, 0.5, la[:, :, j]); r1[:, :, j] = np.where(kd < 2, 4.0, r1[:, :, j]); r2[:, :, j] = 0
    l, u, v = [a[..., m].astype(np.float32) for a in (la, r1, r2)]
    for t in range(RO):
        if t > 0: x = np.roll(x, 1, axis=0); w = np.roll(np.roll(w, -1, axis=0), 1, axis=1)
        y = x + l * (w - x)
        ob[:, :, m, t] = np.where(kd == 3, np.exp2(-rng.integers(80, 111, s)), np.where(kd == 0, y, y - e))
        x = step(np.where(kd < 2, y, x), u, z); w = step(np.where(kd < 2, y, w), v, z)
    return pack(fp, bp, nz, ob, ep, la, r1, r2, p)
def check_ranges(d):
    bad = []
    for k, lo, hi in (("f0", 0, 1), ("b0", 0, 1), ("nz", -0.125, 0.125), ("obs", 0, 1), ("eps", 0, 1), ("lam", 0, 1), ("rf", 0, 4), ("rb", 0, 4), ("pi", 0, K - 1)):
        a = np.asarray(d[k]).astype(np.float64)
        if not (np.min(a) >= lo and np.max(a) <= hi): bad.append("range of " + k)
    x = np.stack([gentries(np.asarray(a)) for a in d["pi"]])
    if not np.array_equal(np.sort(x, axis=-1), np.broadcast_to(np.arange(K), x.shape)): bad.append("pi isn't a permutation in every group")
    return bad
def step(a, r, z):
    return np.minimum(np.maximum(r * (a - a * a) + z, np.float32(0)), np.float32(1))
def reference(f0, b0, nz, obs, eps, lam, rf, rb, pi):
    f = f0.astype(np.float32).reshape(N, 8, 16, S); b = b0.astype(np.float32).reshape(N, 8, 16, S); z = nz.astype(np.float32).reshape(N, 8, 16, S)
    y = obs.astype(np.float32).reshape(N, 8, 16, RO); e, la, r1, r2 = [a.astype(np.float32).reshape(N, 8, 16, 1) for a in (eps, lam, rf, rb)]
    pl = np.stack([gentries(a) for a in pi]).astype(np.int64); ye = []
    for t in range(RO):
        if t > 0:
            f = np.roll(f, 1, axis=0); b = np.roll(np.roll(b, -1, axis=0), 1, axis=1)
        nf, nb = [], []
        for q in range(N):
            yt = y[q, :, :, t:t + 1]; af = ancestors(f[q], yt, e[q]); ab = ancestors(b[q], yt, e[q])
            fi = np.take_along_axis(f[q], af[:, None, :], 2); bj = np.take_along_axis(b[q], np.take_along_axis(ab, pl[q], 1)[:, None, :], 2)
            m = fi + la[q] * (bj - fi)
            ok = np.add.reduce(np.abs(m - yt) <= e[q], axis=1, dtype=np.int64) >= AC
            kf = np.take_along_axis(f[q], af[:, None, ::K // S], 2); kb = np.take_along_axis(b[q], ab[:, None, ::K // S], 2)
            for g in range(8):
                w = np.flatnonzero(ok[g])[:2 * S]; u = w[0::2]; v = w[1::2]
                kf[g, :, :len(u)] = m[g][:, u]; kb[g, :, :len(v)] = m[g][:, v]
            nf.append(step(kf, r1[q], z[q])); nb.append(step(kb, r2[q], z[q]))
            if t == RO - 1:
                d = fi.astype(np.float64) - bj.astype(np.float64)
                ye.append(np.add.reduce(np.exp(-d * d).reshape(8, 16, K // Z, Z), axis=2).reshape(128, Z))
        f = np.stack(nf); b = np.stack(nb)
    return {"yf": f.reshape(N, 128, S).astype(np.float32), "yb": b.reshape(N, 128, S).astype(np.float32), "ye": np.stack(ye).astype(np.float32)}

def check_inputs(d):
    bad = list(check_ranges(d))
    if not bad:
        for name, y in reference(**d).items():
            for q in range(N):
                v = np.abs(np.asarray(y[q], np.float64))
                if v.max() > 4 * np.sqrt(np.mean(v * v)): bad.append('%s of rank %d is uneven' % (name, q))
    return bad

@@ -1,0 +1,606 @@
+from concourse.mybir import AluOpType, ActivationFunctionType
+
+A = AluOpType
+F = ActivationFunctionType
+S, K, RO, Z = 1024, 2048, 4, 256
+f32, b16, u16, i32 = "float32", "bfloat16", "uint16", "int32"
+
+SCRATCH = {}
+
+
+def _sb(name, n, d=f32):
+    SCRATCH[name] = ("sbuf", [128, n], d)
+
+
+for _n in ("f0s", "b0s", "nzs"):
+    _sb(_n, S, b16)
+for _t in (1, 2, 3):
+    _sb("fin%d" % _t, S); _sb("bin%d" % _t, S); _sb("lfi%d" % _t, 128, u16); _sb("lbi%d" % _t, 128, u16)
+for _t in (0, 1):
+    _sb("fo%d" % _t, S); _sb("bo%d" % _t, S)
+    _sb("lfo%d" % _t, 128, u16); _sb("lbo%d" % _t, 128, u16)
+_sb("raw", 8); _sb("par", 8); _sb("parF", 8); _sb("parB", 8); _sb("prm", 12); _sb("pis", 128, i32); _sb("pio", 128, u16)
+_sb("mw", 3 * K); _sb("dd", K); _sb("ab", K); _sb("hh", K, b16); _sb("yes", Z)
+for _p in "fbz":
+    _sb("w" + _p, 128, b16); _sb("cs" + _p, 144); _sb("cb" + _p, 160, b16); _sb("tt" + _p, 64)
+    _sb("low" + _p, 64, b16); _sb("na" + _p, 8); _sb("no" + _p, 8, u16); _sb("zz" + _p, 256, b16); _sb("jo" + _p, 8, u16)
+    _sb("jr" + _p, 136); _sb("aa" + _p, 128)
+for _p in "fb":
+    _sb("sq" + _p, S); _sb("vv" + _p, 1032); _sb("lo" + _p, 64, u16); _sb("rr" + _p, 4); _sb("rho" + _p, 64)
+_sb("junk", 512, b16); _sb("fbk", 132); _sb("nq", 132); _sb("fcn", 132); _sb("js", 128); _sb("seg", 128)
+_sb("sel", 144, b16); _sb("rep", 2048, b16); _sb("itab", 1032); _sb("cr", S, b16); _sb("cla", 128, b16); _sb("clz", 128, b16)
+_sb("ki", 4, i32); _sb("kf", 8); _sb("mrow", 144); _sb("dm", 128, b16); _sb("tmp", 128, b16); _sb("tm2", 128, b16); _sb("same", 128, b16)
+_sb("rc", 16); _sb("amr", 128); _sb("thr", 16); _sb("cq", 128); _sb("ones", 72); _sb("c384", 72, b16); _sb("e0", 128); _sb("e1", 128)
+for _n in ("half", "suf", "two", "me", "mo", "idb", "shb", "off"):
+    _sb(_n, 128, b16)
+for _n in ("pf0", "pf1", "pb0", "pb1", "idf", "shf"):
+    _sb(_n, 128)
+for _k in range(8):
+    SCRATCH["bk%d" % _k] = ("psum", [128, 512], f32)
+
+NDMA = 40
+ARR = ["par0", "par1"] + ["%s%d" % (n, t) for t in (1, 2, 3) for n in ("fa", "fb", "fl", "ba", "bb", "bl")]
+SEMAPHORES = ["pe", "dve", "act", "pool"] + ["d%d" % k for k in range(NDMA)] + ARR
+
+OPT = {"cy": 0.00104, "pec": 0.00052, "hop": 0.10, "fix": 0.06, "ga": 1.56, "tl": 4.0, "ll": 2.0,
+       "pen": 3.0, "look": 0.3, "margin": 0.2, "bb": 2.0, "b0": 3.0, "seed": 0, "amp": 0.0, "nudge": {}, "tries": 1800}
+SETS = [{"hop": 0.1, "fix": 0.05, "pec": 0.00052, "ll": 2.0, "ga": 1.56}, {"hop": 0.2, "fix": 0.03, "pec": 0.0007, "ll": 2.5, "ga": 1.9},
+        {"hop": 0.07, "fix": 0.02, "pec": 0.00052, "ll": 2.0, "ga": 1.2}]
+
+
+def build(T, topo, core):
+    CY, PEC, GA = OPT["cy"], OPT["pec"], OPT["ga"]
+    rank = T.rank_of(core)
+    n = len(T.cores)
+    nxt, prv = T.cores[(rank + 1) % n], T.cores[(rank - 1) % n]
+    ops = []
+    hist = {}
+    lastbank = {}
+    bias = [0.0]
+    site = [0]
+    BOTH = ("act", "dve")
+
+    def add(eng, fn, dur, r=(), w=(), kind="c", lat=0.0, sem=None, cnt=0, after=()):
+        i = len(ops)
+        deps = {}
+        for j in after:
+            deps[j] = "model"
+        for isw, lst in ((False, r), (True, w)):
+            for (nm, lo, hi) in lst:
+                h = hist.setdefault(nm, [])
+                for (j, l2, h2, w2) in h:
+                    if l2 < hi and lo < h2 and (isw or w2) and j != i:
+                        deps[j] = "raw"
+                if nm.startswith("bk"):
+                    j = lastbank.get(nm)
+                    if j is not None and j != i and j not in deps:
+                        deps[j] = "order"
+                    lastbank[nm] = i
+                h.append((i, lo, hi, isw))
+        ops.append({"eng": eng, "fn": fn, "dur": dur, "deps": deps, "kind": kind, "lat": lat, "sem": sem, "cnt": cnt,
+                    "bias": bias[0], "tag": (list(w) + list(r))[0], "site": site[0]})
+        site[0] += 1
+        return i
+
+    def v(nm, lo, hi, step=1, key=None):
+        ap_ = T[nm][:, lo:hi] if step == 1 else T[nm][:, lo:hi:step]
+        return (ap_, (nm, lo, hi) if key is None else key, len(range(lo, hi, step)))
+
+    def ind(win, off):
+        return (win[0].indirect(off[0]), win[1], 16 * off[2], off[1])
+
+    def rs(*xs):
+        out = []
+        for x in xs:
+            if isinstance(x, tuple):
+                out += x[1] if isinstance(x[1], list) else [x[1]]
+                if len(x) > 3:
+                    out.append(x[3])
+        return out
+
+    def ap(x):
+        return x[0] if isinstance(x, tuple) else x
+
+    def cost(n_, k=1.0):
+        return OPT["fix"] + max(64, n_ * k) * CY
+
+    def ts(out, in0, s1, op0, s2=None, op1=None, k=1.0):
+        def fn(q, e):
+            if op1 is None:
+                return q.tensor_scalar(out[0], in0[0], ap(s1), None, op0)
+            return q.tensor_scalar(out[0], in0[0], ap(s1), ap(s2), op0, op1)
+        return add(["dve"], fn, cost(in0[2], k), rs(in0, s1, s2), rs(out))
+
+    def tt(out, in0, in1, op, k=2.0):
+        return add(["dve"], lambda q, e: q.tensor_tensor(out[0], in0[0], in1[0], op), cost(in0[2], k), rs(in0, in1), rs(out))
+
+    def cp(out, in_, k=1.0, eng=("dve",)):
+        def fn(q, e):
+            if e == "dve":
+                return q.tensor_copy(out[0], in_[0])
+            return q.activation(out[0], in_[0], F.Copy)
+        return add(list(eng), fn, cost(in_[2], k), rs(in_), rs(out))
+
+    def mul(out, in_, c, eng=("act",)):
+        def fn(q, e):
+            if e == "dve":
+                return q.tensor_scalar(out[0], in_[0], ap(c), None, A.mult)
+            return q.activation(out[0], in_[0], F.Identity, scale=ap(c))
+        return add(list(eng), fn, cost(in_[2]), rs(in_, c), rs(out))
+
+    def lin(out, in_, scale, bias_):
+        def fn(q, e):
+            if e == "dve":
+                return q.tensor_scalar(out[0], in_[0], ap(scale), bias_, A.mult, A.add)
+            return q.activation(out[0], in_[0], F.Identity, bias=bias_, scale=ap(scale))
+        return add(list(BOTH), fn, cost(in_[2]), rs(in_, scale), rs(out))
+
+    def act(out, in_, func, bias=0.0, scale=1.0, acc=None, k=1.0, extra=0.0):
+        def fn(q, e):
+            if acc is None:
+                return q.activation(out[0], in_[0], func, bias=ap(bias), scale=ap(scale))
+            return q.activation(out[0], in_[0], func, bias=ap(bias), scale=ap(scale), accum_out=acc[0])
+        return add(["act"], fn, cost(in_[2], k) + extra, rs(in_, bias, scale), rs(out, acc))
+
+    def scan(out, d0, d1, init, op0, op1):
+        return add(["dve"], lambda q, e: q.tensor_tensor_scan(out[0], d0[0], d1[0], ap(init), op0, op1), cost(out[2]), rs(d0, d1, init), rs(out))
+
+    def ms(out, c, k=1.0):
+        return add(["dve"], lambda q, e: q.memset(out[0], c), cost(out[2], k), [], rs(out))
+
+    def mms(items, k=1):
+        def fn(q, e):
+            return [q.matmul(o[0], l[0], r[0], st, sp) for (o, l, r, st, sp) in items][-1]
+        return add(["pe"], fn, sum(0.004 + max(64, x[2][2]) * k * PEC for x in items), [y for x in items for y in rs(x[1], x[2])], [y for x in items for y in rs(x[0])])
+
+    def iota(out, pat, base, cm, integer=False):
+        def fn(q, e):
+            if integer:
+                return q.iota(out[0], pat, base, cm)
+            return q.iota(out[0], pat, base, cm, allow_small_or_imprecise_dtypes=True)
+        return add(["pool"], fn, 0.13 + 2 * CY * out[2], [("poolq", 0, 1)], rs(out) + [("poolq", 0, 1)])
+
+    nd = [0]
+
+    def dsem():
+        nd[0] += 1
+        return "d%d" % (nd[0] - 1)
+
+    def dma(q_, out, in_, lat, r=(), w=()):
+        return add([q_], lambda q, e: q.dma_start(out, in_), 0.06, r, w, kind="dma", lat=lat, sem=dsem(), cnt=16)
+
+    narrow = min((topo.engines(core, d) for d in (nxt, prv)), key=len)
+    emask = {}
+    for d in (nxt, prv):
+        es = topo.engines(core, d)
+        rest = [e for e in es if e not in narrow]
+        emask[d] = rest if rest else es
+
+    def send(dst, out, in_, rsem, lat):
+        rid, pid = topo.addr(dst, core)
+        es = emask[dst]
+        m = sum(1 << e for e in es)
+        ls = dsem()
+        i = add(["pool"], lambda q, e: q.remote_dma(out[0], in_[0], T.sem[rsem], T.sem[ls], pid, rid, m), 0.5, rs(in_), [],
+                kind="dma", lat=lat, sem=ls, cnt=len(es))
+        add([None], None, 0.0, [], rs(out), kind="arr", lat=lat, sem=rsem, cnt=len(narrow), after=[i])
+
+    def bank(k_, lo, hi, step=1):
+        return v("bk%d" % k_, lo, hi, step)
+
+    def col(nm, c):
+        return v(nm, c, c + 1)
+
+    def mat(nm):
+        return v(nm, 0, 128)
+
+    def rows(nm, p0, p1, key, width):
+        return (T[nm][p0:p1, :], (nm, key, key + 1), width)
+
+    dma("sp", T.b0s[:], T.b0[:], 2.6, w=[("b0s", 0, S)])
+    dma("act", T.raw[:, 0:4], T.obs[:], 2.0, w=[("raw", 0, 4)])
+    dma("act", T.raw[:, 4:5], T.eps[:], 2.0, w=[("raw", 4, 5)])
+    dma("sp", T.f0s[:], T.f0[:], 3.0, w=[("f0s", 0, S)])
+    dma("sp", T.pis[:], T.pi[:], 3.0, w=[("pis", 0, 128)])
+    dma("sp", T.prm[:, 0:1], T.lam[:], 3.0, w=[("prm", 0, 1)])
+    dma("sp", T.prm[:, 4:5], T.rf[:], 3.0, w=[("prm", 4, 5)])
+    dma("sp", T.prm[:, 8:9], T.rb[:], 3.0, w=[("prm", 8, 9)])
+    dma("sp", T.nzs[:], T.nz[:], 3.0, w=[("nzs", 0, S)])
+    lam, rate = col("prm", 0), {"f": col("prm", 4), "b": col("prm", 8)}
+
+    iota(v("ki", 0, 1), [[0, 1]], 0, 1, integer=True)
+    iota(v("mrow", 0, 144), [[1, 144]], 0, 0)
+    ts(col("ki", 1), col("ki", 0), 15, A.bitwise_and)
+    cp(v("kf", 0, 2), v("ki", 0, 2))
+    kk, ak = col("kf", 0), col("kf", 1)
+    tt(col("kf", 2), kk, ak, A.subtract)
+    bias[0] = 20.0
+    ts(mat("dm"), mat("mrow"), col("kf", 2), A.subtract)
+    dm = mat("dm")
+    ts(mat("tmp"), dm, -0.5, A.is_gt, k=0.5)
+    ts(mat("tm2"), dm, 15.5, A.is_lt, k=0.5)
+    tt(mat("same"), mat("tmp"), mat("tm2"), A.mult, k=1)
+    same = mat("same")
+    ts(v("rc", 0, 16), v("mrow", 0, 16), ak, A.is_equal, -65536.0, A.mult)
+    bias[0] = 0.0
+    ts(v("sel", 0, 144), v("mrow", 0, 144), col("kf", 2), A.subtract, 15.0, A.is_equal)
+    mul(mat("half"), same, 0.5)
+    ts(mat("tmp"), dm, ak, A.is_lt, 0.5, A.mult, k=0.5)
+    tt(mat("suf"), mat("tmp"), same, A.mult, k=1)
+    ms(v("c384", 0, 72), -384.0); ms(v("ones", 0, 64), 1.0); ms(v("ones", 64, 65), 1.0 / 128)
+    for p in "fb":
+        ms(v("w" + p, 64, 65), 384.0); ms(v("vv" + p, 0, 1), 0.0); ms(v("jr" + p, 0, 1), 0.0)
+    for p in "fbz":
+        ms(v("cb" + p, 144, 160), 1024.0)
+    for a in range(16):
+        mul(v("rep", 128 * a, 128 * a + 128), same, col("rc", a))
+    ts(v("par", 0, 4), v("raw", 0, 4), -1.0, A.mult)
+    cp(v("par", 4, 8), v("raw", 1, 5))
+    send(prv, v("parF", 0, 8), v("par", 0, 8), "par0", 3.0)
+    send(nxt, v("parB", 0, 8), v("par", 0, 8), "par1", 3.0)
+    iota(v("itab", 0, 1025), [[1, 1025]], 0, 0)
+    ms(rows("cr", 0, 32, 0, S), 2048.0, 0.5); ms(rows("cr", 96, 128, 3, S), 2048.0, 0.5)
+    iota(rows("cr", 32, 64, 1, S), [[16, 64], [0, 16]], 0, 0)
+    iota(rows("cr", 64, 96, 2, S), [[0, 64], [2, 16]], 1, 0)
+    iota(mat("amr"), [[0, 8], [2, 16]], 1, 0)
+    mul(rows("cla", 0, 32, 0, 128), (T.amr[0:32, :], ("amr", 0, 128), 128), 1.0 / 32)
+    mul(rows("clz", 0, 32, 0, 128), (T.amr[0:32, :], ("amr", 0, 128), 128), 1.0)
+    for nm, lastc in (("cla", 12.0), ("clz", 0.0)):
+        for (p0, c, key) in ((32, 1.0 / 32, 1), (64, 1.0 / 64, 2), (96, lastc, 3)):
+            ms(rows(nm, p0, p0 + 32, key, 64), c)
+    ts(v("thr", 0, 8), v("mrow", 0, 128, 16), ak, A.add, 129.5, A.add)
+    ts(v("thr", 8, 16), v("thr", 0, 8), -128.515625, A.add, 32.0, A.mult)
+    lin(mat("cq"), mat("mrow"), 1.0, 129.5)
+    ts(mat("idf"), dm, ak, A.is_equal)
+    mul(mat("idb"), mat("idf"), 1.0)
+    ts(col("kf", 4), ak, 2.0, A.mult)
+    ts(mat("e0"), mat("amr"), col("kf", 4), A.subtract, 1.0, A.not_equal)
+    mul(mat("off"), mat("e0"), -8192.0)
+    ts(mat("seg"), mat("amr"), 1.0, A.is_equal, -4096.0, A.mult)
+    cp(mat("pio"), mat("pis"))
+    mul(mat("two"), same, 2.0)
+    ts(mat("e0"), dm, -2.0, A.mult, ak, A.add)
+    lin(mat("e1"), mat("e0"), 1.0, 16.0)
+    for nm, e_, t_ in (("me", "e0", "tmp"), ("mo", "e1", "tm2")):
+        ts(mat(t_), mat(e_), 0.0, A.max, 2.0, A.min)
+        tt(mat(nm), mat(t_), same, A.mult, k=1)
+    for nm, e_, c in (("pf0", "e0", 0.0), ("pf1", "e1", 0.0), ("pb0", "e0", 1.0), ("pb1", "e1", 1.0)):
+        ts(mat(nm), mat(e_), c, A.is_equal, 2.0, A.mult)
+    ts(col("ki", 2), col("ki", 0), 16.0, A.add)
+    ts(col("ki", 3), col("ki", 2), 127, A.bitwise_and)
+    cp(col("kf", 3), col("ki", 3))
+    ts(mat("shf"), mat("mrow"), col("kf", 3), A.is_equal)
+    mul(mat("shb"), mat("shf"), 1.0)
+    ts(v("nq", 0, 129), v("mrow", 0, 129), 32.0, A.mult, col("kf", 4), A.add)
+    ts(col("ki", 2), col("ki", 0), 1, A.bitwise_and)
+    cp(col("kf", 5), col("ki", 2))
+    ts(col("kf", 6), col("kf", 5), 1023.5, A.mult, 1024.0, A.add)
+    ts(v("fcn", 0, 129), v("nq", 0, 129), 0.25, A.mult, col("kf", 6), A.add)
+
+    def umat(p, ub):
+        cl = "clz" if p == "z" else "cla"
+        for h in (0, 1):
+            mms([(bank(ub[h], 0, 512), v(cl, 0, 128, key=(cl, 0, 4)), v("cr", 512 * h, 512 * h + 512, key=("cr", 0, 4)), True, False)])
+
+    def invert(p, vp, ub, sb, lvl1, thr0):
+        V, zz, no, jo = "vv" + vp, "zz" + p, v("no" + p, 0, 8), v("jo" + p, 0, 8)
+        for cc in range(8):
+            act(v("junk", 64 * cc, 64 * cc + 64), lvl1, F.Sign, bias=col("thr", thr0 + cc), scale=-1.0, acc=col("na" + p, cc))
+        ts(no, v("na" + p, 0, 8), 0.5, A.mult, 32.0, A.add)
+        tt(v(zz, 0, 128), ind(v("cb" + p, 80, 160), no), mat("cq"), A.is_lt, k=GA)
+        cp(v(zz, 128, 256), ind(v("itab", 0, 72), no), k=GA, eng=("act",))
+        for h in (0, 1):
+            mms([(bank(ub[h], a, 512, 16), v("rep", 128 * a, 128 * a + 128), v("low" + p, 32 * h, 32 * h + 32), False, a == 15) for a in range(16)])
+        mms([(bank(sb, 0, 128), mat("idb"), mat("off"), True, False), (bank(sb, 0, 128), same, v(zz, 128, 256), False, False), (bank(sb, 0, 128), same, v(zz, 0, 128), False, True),
+             (bank(sb, 128, 256), same, v(zz, 128, 256), True, False), (bank(sb, 128, 256), same, v(zz, 0, 128), False, True)])
+        scan(mat("js"), mat("seg"), bank(sb, 0, 128), 0.0, A.add, A.max)
+        cp(jo, v("js", 15, 128, 16))
+        if p == "z":
+            ts(v("fbk", 0, 129), v("nq", 0, 129), col("csz", 127), A.is_ge)
+            tt(v("jrz", 0, 129), v("fbk", 0, 129), v("fcn", 0, 129), A.mult)
+            tt(v("jrz", 1, 129), v("jrz", 1, 129), bank(sb, 128, 256), A.max, k=1)
+        else:
+            cp(v("jr" + p, 1, 129), bank(sb, 128, 256), eng=BOTH)
+        for h in (0, 1):
+            scan(v(V, 1 + 512 * h, 513 + 512 * h), bank(ub[h], 0, 512), v("itab", 1 + 512 * h, 513 + 512 * h), col(V, 512 * h), A.max, A.min)
+        tt(mat("aa" + p), ind(v(V, 0, 1025), jo), v("jr" + p, 0, 128), A.max, k=GA)
+
+    def hits(x, xo, o, prm, t, split):
+        for e in ((0, 1) if split else (None,)):
+            st, d = (1, 0) if e is None else (2, e)
+            keys = [[(nm + s_, o, o + 512) for s_ in ("01" if e is None else str(e))] for nm in ("ab", "hh")]
+            a_ = v("ab", o + d, o + 512, st, key=keys[0])
+            act(a_, v(x, xo + d, xo + 512, st), F.Abs, bias=col(prm, t))
+            ts(v("hh", o + d, o + 512, st, key=keys[1]), a_, col(prm, 7), A.is_le)
+
+    def counts(sb, c0, o):
+        for e in (0, 1):
+            mms([(bank(sb, c0, c0 + 64), v("sel", 15 - a, 143 - a), v("hh", o + a, o + S, 16, key=("hh%d" % e, o, o + S)), a == 0, a == 15) for a in range(e, 16, 2)])
+
+    def ancestors(p, x, prm, t, lst, ub, sb, o):
+        hits(x, 0, o, prm, t, False)
+        hits(x, 512, o + 512, prm, t, True)
+        umat(p, ub)
+        counts(sb, 0, o)
+        ts(v("w" + p, 0, 64), bank(sb, 0, 64), 2.0, A.max, 383.75, A.add)
+        mms([(bank(sb, 128, 193), mat("half"), v("c384", 0, 65), True, False), (bank(sb, 128, 193), mat("half"), v("w" + p, 0, 65), False, True),
+             (bank(sb, 200, 264), mat("suf"), v("c384", 0, 64), True, False), (bank(sb, 200, 264), mat("suf"), v("w" + p, 0, 64), False, True)])
+        cs = "cs" + p
+        scan(v(cs, 15, 80), v("ones", 0, 65), bank(sb, 128, 193), 0.0, A.mult, A.add)
+        add(["dve"], lambda q, e: q.reciprocal(T["rr" + p][:, 0:1], T[cs][:, 79:80]), 0.25, [(cs, 79, 80)], [("rr" + p, 0, 1)])
+        r = col("rr" + p, 0)
+        tt(v(cs, 80, 144), v(cs, 15, 79), bank(sb, 200, 264), A.subtract, k=1)
+        lin(v("cb" + p, 15, 144), v(cs, 15, 144), r, 128.53125)
+        ts(v("tt" + p, 0, 64), v("cb" + p, 80, 144), -129.0, A.add, col(cs, 79), A.mult)
+        tt(v("rho" + p, 0, 64), v(cs, 80, 144), v("tt" + p, 0, 64), A.subtract)
+        lin(v("low" + p, 0, 64), v("rho" + p, 0, 64), r, 12.0 + (0.5 - 2.0 ** -14) / 16)
+        invert(p, p, ub, sb, v("cb" + p, 15, 79), 0)
+        cp(mat(lst), mat("aa" + p))
+
+    bias[0] = OPT["b0"]
+    ancestors("b", "b0s", "par", 0, "lbo0", (4, 5), 6, 0)
+    bias[0] = 0.0
+    ancestors("f", "f0s", "par", 0, "lfo0", (0, 1), 7, S)
+    for t in range(RO):
+        last = t == RO - 1
+        site[0] = 2000 if last else 1000
+        bias[0] = 0.0
+        fw, bw, lf, lb = ("f0s", "b0s", "lfo0", "lbo0") if t == 0 else ("fin%d" % t, "bin%d" % t, "lfi%d" % t, "lbi%d" % t)
+        for c in range(4):
+            cp(v("mw", 2 * K + 512 * c, 2 * K + 512 * c + 512), ind(v(bw, 0, S), v(lb, 32 * c, 32 * c + 32)), k=GA, eng=BOTH)
+        for c in range(4):
+            cp(v("mw", K + 512 * c, K + 512 * c + 512), ind(v(fw, 0, S), v(lf, 32 * c, 32 * c + 32)), k=GA, eng=BOTH if c == 0 else ("act",))
+        umat("z", (4, 5))
+        for c in range(4):
+            lo, hi = 512 * c, 512 * c + 512
+            fi = v("mw", K + lo, K + hi)
+            tt(v("dd", lo, hi), ind(v("mw", 2 * K, 3 * K), v("pio", 32 * c, 32 * c + 32)), fi, A.subtract, k=GA)
+            mul(bank(c % 2, 0, 512), v("dd", lo, hi), lam)
+            tt(v("mw", lo, hi), fi, bank(c % 2, 0, 512), A.add, k=1)
+            hits("mw", lo, lo, "par", t, c == 3)
+            if c % 2:
+                counts(6, 64 * (c // 2), S * (c // 2))
+        ts(mat("wz"), bank(6, 0, 128), 8.5, A.is_ge)
+        we, wo = v("wz", 0, 128, 2), v("wz", 1, 128, 2)
+        mms([(bank(6, 128, 192), mat("two"), we, True, False), (bank(6, 128, 192), mat("two"), wo, False, True),
+             (bank(6, 200, 264), mat("me"), we, True, False), (bank(6, 200, 264), mat("mo"), wo, False, True)])
+        scan(v("csz", 64, 128), v("ones", 0, 64), bank(6, 128, 192), 0.0, A.mult, A.add)
+        tt(v("csz", 0, 64), v("csz", 64, 128), bank(6, 200, 264), A.subtract, k=1)
+        lin(v("cbz", 80, 144), v("csz", 0, 64), 1.0 / 32, 128.515625)
+        lin(v("ttz", 0, 64), v("cbz", 80, 144), 32.0, -129.0 * 32)
+        tt(v("lowz", 0, 64), v("csz", 0, 64), v("ttz", 0, 64), A.subtract)
+        invert("z", "b", (4, 5), 6, v("csz", 64, 128), 8)
+        if last:
+            for c in range(4):
+                x = v("dd", 512 * c, 512 * c + 512)
+                act(x, x, F.Square)
+                act(x, x, F.Exp, scale=-1.0, extra=1.3 if c == 0 else 0.0)
+                mms([(bank(7, 0, Z), mat("idf"), v("dd", Z * j, Z * j + Z), j == 0, j == 7) for j in (2 * c, 2 * c + 1)], k=4)
+            cp(v("yes", 0, Z), bank(7, 0, Z), eng=BOTH)
+            dma("sp", T.ye[:], T.yes[:], 2.2, r=[("yes", 0, Z)])
+        for p, sb in (("b", 6), ("f", 2)):
+            mms([(bank(sb, 288, 352), mat("p%s0" % p), v("aaz", 0, 128, 2), True, False), (bank(sb, 288, 352), mat("p%s1" % p), v("aaz", 1, 128, 2), False, True)], k=4)
+            cp(v("lo" + p, 0, 64), bank(sb, 288, 352))
+        for p, pb in (("b", (0, 1)), ("f", (2, 3))):
+            po = "%so%d" % (p, t % 2)
+            bias[0] = OPT["bb"] if p == "b" else 0.0
+            sh = p == "b" and not last
+            dst = prv if p == "b" else nxt
+            for h in (0, 1):
+                lo, hi = 512 * h, 512 * h + 512
+                hv = ind(v("mw", 0, 3 * K if p == "b" else 2 * K), v("lo" + p, 32 * h, 32 * h + 32))
+                x = v("sq" + p, lo, hi)
+                mms([(bank(pb[h], 0, 512), mat("shb" if sh else "idb"), v("nzs", lo, hi), True, False)])
+                act(x, hv, F.Square, k=GA)
+                tt(x, hv, x, A.subtract, k=GA)
+                mul(x, x, rate[p])
+                mms([(bank(pb[h], 0, 512), mat("shf" if sh else "idf"), x, False, True)], k=4)
+                ts(v(po, lo, hi), bank(pb[h], 0, 512), 0.0, A.max, 1.0, A.min)
+                if last:
+                    dma("sp", T["y" + p][:, lo:hi], T[po][:, lo:hi], 2.4, r=[(po, lo, hi)])
+                else:
+                    send(dst, v("%sin%d" % (p, t + 1), lo, hi), v(po, lo, hi), "%s%s%d" % (p, "ab"[h], t + 1), OPT["tl"] * (1 + h / 4))
+            if not last:
+                lst = "l%so%d" % (p, (t + 1) % 2)
+                ancestors(p, po, "parB" if p == "b" else "parF", t + 1, lst, (4, 5) if p == "b" else (0, 1), 6 if p == "b" else 7, 0 if p == "b" else S)
+                send(dst, mat("l%si%d" % (p, t + 1)), mat(lst), "%sl%d" % (p, t + 1), OPT["ll"])
+    return ops
+
+
+def schedule(ops):
+    HOP = OPT["hop"]
+    n = len(ops)
+    succ = [[] for _ in range(n)]
+    for i, o in enumerate(ops):
+        for j in o["deps"]:
+            succ[j].append(i)
+    prio = [0.0] * n
+    for i in range(n - 1, -1, -1):
+        prio[i] = ops[i]["dur"] + ops[i]["lat"] + max([prio[j] + HOP for j in succ[i]] + [0.0])
+    x = OPT["seed"]
+    for i in range(n):
+        x = (x * 1103515245 + 12345) % 2147483648
+        prio[i] += ops[i]["bias"] + OPT["amp"] * (x / 2147483648.0) + OPT["nudge"].get(ops[i]["site"], 0.0)
+    left = [len(o["deps"]) for o in ops]
+    cand = [i for i in range(n) if left[i] == 0]
+    free = {e: 0.0 for e in ("pe", "dve", "act", "pool", "sp")}
+    order = []
+    memo = {}
+
+    def ready(i, e):
+        if (i, e) not in memo:
+            r = 0.0
+            for j, kd in ops[i]["deps"].items():
+                o = ops[j]
+                if kd == "model" or (o["kind"] == "c" and o["on"] == e and (kd == "order" or e == "pe")):
+                    r = max(r, o["end"])
+                else:
+                    r = max(r, o["done"] + HOP)
+            memo[(i, e)] = r
+        return memo[(i, e)]
+
+    def place(i, e, st):
+        o = ops[i]
+        o["on"] = e; o["start"] = st; o["end"] = st + o["dur"]; o["done"] = o["end"] + o["lat"]
+        if e is not None:
+            free[e] = o["end"]
+        order.append(i)
+        cand.remove(i)
+        for j in succ[i]:
+            left[j] -= 1
+            if left[j] == 0:
+                cand.append(j)
+
+    while cand:
+        arr = [i for i in cand if ops[i]["kind"] == "arr"]
+        if arr:
+            place(arr[0], None, ready(arr[0], None))
+            continue
+        opts = [(max(free[e], ready(i, e)), i, e) for i in cand for e in ops[i]["eng"]]
+        t0, _, e0 = min(opts)
+        def rank_(y):
+            return (prio[y[1]] - (OPT["pen"] if len(ops[y[1]]["eng"]) > 1 and y[2] == "dve" else 0.0), -y[1])
+        now = [y for y in opts if y[2] == e0 and y[0] <= t0 + 1e-9]
+        b = max(now, key=rank_)
+        soon = [y for y in opts if y[2] == e0 and t0 + 1e-9 < y[0] < t0 + OPT["look"] * ops[b[1]]["dur"] and rank_(y)[0] > rank_(b)[0] + OPT["margin"]]
+        if soon:
+            u = max(soon, key=rank_)
+            fit = [y for y in now if ops[y[1]]["dur"] <= u[0] - t0 + 0.03]
+            b = max(fit, key=rank_) if fit else u
+        place(b[1], b[2], b[0])
+    return order
+
+
+def replay(ops, order, on, hop):
+    free = {}
+    end = [0.0] * len(ops)
+    for i in order:
+        o, e = ops[i], on[i]
+        r = free.get(e, 0.0) if e else 0.0
+        for j, kd in o["deps"].items():
+            d = ops[j]
+            r = max(r, end[j] if kd == "model" or (d["kind"] == "c" and on[j] == e and (kd == "order" or e == "pe")) else end[j] + d["lat"] + hop)
+        end[i] = r + o["dur"]
+        if e:
+            free[e] = end[i]
+    return max(end[i] + o["lat"] for i, o in enumerate(ops))
+
+
+def tune(T, topo, core):
+    base = dict(OPT)
+    ops = build(T, topo, core)
+    alts = []
+    for s in SETS:
+        OPT.update(s)
+        alts.append(build(T, topo, core))
+        OPT.update(base)
+    sites = sorted({o["site"] for o in ops if o["kind"] != "arr"})
+    x = [12345]
+
+    def pick(seq):
+        x[0] = (x[0] * 1103515245 + 12345) % 2147483648
+        return seq[(x[0] >> 8) % len(seq)]
+
+    def score(nudge):
+        OPT["nudge"] = nudge
+        order = schedule(ops)
+        on = [o["on"] for o in ops]
+        return sum(replay(a, order, on, s["hop"]) for a, s in zip(alts, SETS))
+    cur = {}
+    best = score(cur)
+    for _ in range(OPT["tries"]):
+        c = dict(cur)
+        for _k in range(pick((1, 2, 4, 8))):
+            a, d = pick(range(len(sites))), pick((-3, -1.5, -0.7, -0.3, 0.3, 0.7, 1.5, 3))
+            for y in sites[a:a + pick((1, 1, 2, 4, 8))]:
+                c[y] = c.get(y, 0.0) + d
+        s = score(c)
+        if s < best - 0.03:
+            best, cur = s, c
+    OPT["nudge"] = cur
+    OPT["tries"] = 0
+    OPT["best"] = best / len(SETS)
+
+
+def rank_program(g, core, T, topo):
+    if T.rank_of(core) is None:
+        return
+    if OPT["tries"]:
+        tune(T, topo, core)
+    ops = build(T, topo, core)
+    order = schedule(ops)
+    Q = {"pe": g.tensor, "dve": g.vector, "act": g.scalar, "pool": g, "sp": g.sync}
+
+    def waits(i):
+        o = ops[i]
+        out = []
+        for j, kd in o["deps"].items():
+            d = ops[j]
+            if kd == "model":
+                continue
+            if d["kind"] == "c" and o["kind"] == "c" and d["on"] == o["on"] and (kd == "order" or o["on"] == "pe"):
+                continue
+            out.append(j)
+        return out
+
+    pos = {}
+    seen = {e: 0 for e in Q}
+    for i in order:
+        if ops[i]["kind"] == "c":
+            seen[ops[i]["on"]] += 1
+            pos[i] = seen[ops[i]["on"]]
+    know = {e: {} for e in Q}
+    after = {}
+    need = {}
+    signal = set()
+    for i in order:
+        o = ops[i]
+        if o["kind"] == "arr":
+            after[i] = {o["sem"]: 1}
+            continue
+        kn = know[o["on"]]
+        lst = []
+        for j in sorted(waits(i), key=lambda j: -ops[j]["done"]):
+            d = ops[j]
+            key, val = (d["on"], pos[j]) if d["kind"] == "c" else (d["sem"], 1)
+            if kn.get(key, 0) >= val:
+                continue
+            lst.append(j)
+            signal.add(j)
+            for k_, x in after[j].items():
+                if kn.get(k_, 0) < x:
+                    kn[k_] = x
+        need[i] = lst
+        a = dict(kn)
+        if o["kind"] == "c":
+            a[o["on"]] = pos[i]
+        else:
+            a[o["sem"]] = 1
+        after[i] = a
+    count = {e: 0 for e in Q}
+    val = {}
+    for i in order:
+        o = ops[i]
+        if o["kind"] == "arr":
+            continue
+        e = o["on"]
+        for j in need[i]:
+            d = ops[j]
+            if d["kind"] == "c":
+                Q[e].wait_ge(T.sem[d["on"]], val[j])
+            else:
+                Q[e].wait_ge(T.sem[d["sem"]], d["cnt"])
+        ins = o["fn"](Q[e], e)
+        if o["kind"] == "c":
+            if i in signal:
+                count[e] += 1
+                val[i] = count[e]
+                ins.then_inc(T.sem[e], 1)
+        elif e != "pool":
+            ins.then_inc(T.sem[o["sem"]], 16)
+    for o in ops:
+        if o["kind"] != "c":
+            g.wait_ge(T.sem[o["sem"]], o["cnt"])
+    for e in ("pe", "dve", "act", "pool"):
+        if count[e]:
+            g.wait_ge(T.sem[e], count[e])

@@ -14,12 +14,12 @@ def _sb(name, n, d=f32):
 
 for _n in ("f0s", "b0s", "nzs"):
     _sb(_n, S, b16)
-for _t in (1, 2, 3):
-    _sb("fin%d" % _t, S); _sb("bin%d" % _t, S); _sb("lfi%d" % _t, 128, u16); _sb("lbi%d" % _t, 128, u16)
+for _n in ("b%s1", "f%s2", "f%s3", "b%s3"):
+    _sb(_n % "in", S); _sb("l" + _n % "i", 128, u16)
 for _t in (0, 1):
     _sb("fo%d" % _t, S); _sb("bo%d" % _t, S)
     _sb("lfo%d" % _t, 128, u16); _sb("lbo%d" % _t, 128, u16)
-_sb("raw", 8); _sb("par", 8); _sb("parF", 8); _sb("parB", 8); _sb("prm", 12); _sb("pis", 128, i32); _sb("pio", 128, u16)
+_sb("raw", 8); _sb("par", 8); _sb("parF", 8); _sb("parB", 8); _sb("parO", 8); _sb("nzn", S, b16); _sb("pin", 128, u16); _sb("pis", 128, i32); _sb("pio", 128, u16)
 _sb("mw", 3 * K); _sb("dd", K); _sb("ab", K); _sb("hh", K, b16); _sb("yes", Z)
 for _p in "fbz":
     _sb("w" + _p, 128, b16); _sb("cs" + _p, 144); _sb("cb" + _p, 160, b16); _sb("tt" + _p, 64)
@@ -38,14 +38,16 @@ for _n in ("pf0", "pf1", "pb0", "pb1", "idf", "shf"):
 for _k in range(8):
     SCRATCH["bk%d" % _k] = ("psum", [128, 512], f32)
 
-NDMA = 40
-ARR = ["par0", "par1"] + ["%s%d" % (n, t) for t in (1, 2, 3) for n in ("fa", "fb", "fl", "ba", "bb", "bl")]
+NDMA = 48
+ARR = ["par0", "par1", "par2", "nzn", "pin"] + [n % k for n in ("b%s1", "f%s2", "f%s3", "b%s3") for k in "abl"]
 SEMAPHORES = ["pe", "dve", "act", "pool"] + ["d%d" % k for k in range(NDMA)] + ARR
 
-OPT = {"cy": 0.00104, "pec": 0.00052, "hop": 0.10, "fix": 0.06, "ga": 1.56, "tl": 4.0, "ll": 2.0,
-       "pen": 3.0, "look": 0.3, "margin": 0.2, "bb": 2.0, "b0": 3.0, "seed": 0, "amp": 0.0, "nudge": {}, "tries": 1800}
-SETS = [{"hop": 0.1, "fix": 0.05, "pec": 0.00052, "ll": 2.0, "ga": 1.56}, {"hop": 0.2, "fix": 0.03, "pec": 0.0007, "ll": 2.5, "ga": 1.9},
-        {"hop": 0.07, "fix": 0.02, "pec": 0.00052, "ll": 2.0, "ga": 1.2}]
+OPT = {"cy": 0.00083, "pec": 0.00042, "hop": 0.2, "fix": 0.02, "ga": 1.56, "tl": 4.0, "ll": 2.0,
+       "pen": 3.0, "first": 380, "span": 5.0, "back": 0.5, "look": 0.3, "margin": 0.2, "bb": 2.0, "bs": 3.0, "b0": 3.0, "seed": 0, "amp": 2.5,
+       "nudge": {}, "force": {}, "tries": 3000, "cuts": (0, 512, 1024, 1536, 2048),
+       "sc": ((0, 256, 512, 1024), (0, 512, 1024)), "scl": ((0, 512, 1024), (0, 512, 768, 1024))}
+SETS = [{"cy": 0.00083, "hop": 0.2, "fix": 0.02, "pec": 0.00042, "ll": 2.0, "ga": 1.56},
+        {"cy": 0.0012, "hop": 0.22, "fix": 0.03, "pec": 0.0006, "ll": 3.0, "tl": 6.0, "ga": 2.0}]
 
 
 def build(T, topo, core):
@@ -53,6 +55,7 @@ def build(T, topo, core):
     rank = T.rank_of(core)
     n = len(T.cores)
     nxt, prv = T.cores[(rank + 1) % n], T.cores[(rank - 1) % n]
+    opp = T.cores[(rank + 2) % n]
     ops = []
     hist = {}
     lastbank = {}
@@ -131,9 +134,9 @@ def build(T, topo, core):
     def lin(out, in_, scale, bias_):
         def fn(q, e):
             if e == "dve":
-                return q.tensor_scalar(out[0], in_[0], ap(scale), bias_, A.mult, A.add)
-            return q.activation(out[0], in_[0], F.Identity, bias=bias_, scale=ap(scale))
-        return add(list(BOTH), fn, cost(in_[2]), rs(in_, scale), rs(out))
+                return q.tensor_scalar(out[0], in_[0], ap(scale), ap(bias_), A.mult, A.add)
+            return q.activation(out[0], in_[0], F.Identity, bias=ap(bias_), scale=ap(scale))
+        return add(list(BOTH), fn, cost(in_[2]), rs(in_, scale, bias_), rs(out))
 
     def act(out, in_, func, bias=0.0, scale=1.0, acc=None, k=1.0, extra=0.0):
         def fn(q, e):
@@ -171,7 +174,7 @@ def build(T, topo, core):
 
     narrow = min((topo.engines(core, d) for d in (nxt, prv)), key=len)
     emask = {}
-    for d in (nxt, prv):
+    for d in (nxt, prv, opp):
         es = topo.engines(core, d)
         rest = [e for e in es if e not in narrow]
         emask[d] = rest if rest else es
@@ -199,14 +202,13 @@ def build(T, topo, core):
 
     dma("sp", T.b0s[:], T.b0[:], 2.6, w=[("b0s", 0, S)])
     dma("act", T.raw[:, 0:4], T.obs[:], 2.0, w=[("raw", 0, 4)])
-    dma("act", T.raw[:, 4:5], T.eps[:], 2.0, w=[("raw", 4, 5)])
+    dma("act", T.raw[:, 7:8], T.eps[:], 2.0, w=[("raw", 7, 8)])
     dma("sp", T.f0s[:], T.f0[:], 3.0, w=[("f0s", 0, S)])
     dma("sp", T.pis[:], T.pi[:], 3.0, w=[("pis", 0, 128)])
-    dma("sp", T.prm[:, 0:1], T.lam[:], 3.0, w=[("prm", 0, 1)])
-    dma("sp", T.prm[:, 4:5], T.rf[:], 3.0, w=[("prm", 4, 5)])
-    dma("sp", T.prm[:, 8:9], T.rb[:], 3.0, w=[("prm", 8, 9)])
+    dma("sp", T.raw[:, 4:5], T.lam[:], 3.0, w=[("raw", 4, 5)])
+    dma("sp", T.raw[:, 5:6], T.rf[:], 3.0, w=[("raw", 5, 6)])
+    dma("sp", T.raw[:, 6:7], T.rb[:], 3.0, w=[("raw", 6, 7)])
     dma("sp", T.nzs[:], T.nz[:], 3.0, w=[("nzs", 0, S)])
-    lam, rate = col("prm", 0), {"f": col("prm", 4), "b": col("prm", 8)}
 
     iota(v("ki", 0, 1), [[0, 1]], 0, 1, integer=True)
     iota(v("mrow", 0, 144), [[1, 144]], 0, 0)
@@ -227,27 +229,29 @@ def build(T, topo, core):
     mul(mat("half"), same, 0.5)
     ts(mat("tmp"), dm, ak, A.is_lt, 0.5, A.mult, k=0.5)
     tt(mat("suf"), mat("tmp"), same, A.mult, k=1)
-    ms(v("c384", 0, 72), -384.0); ms(v("ones", 0, 64), 1.0); ms(v("ones", 64, 65), 1.0 / 128)
+    ms(v("c384", 0, 72), -384.0); ms(v("ones", 0, 64), 1.0); ms(v("ones", 64, 65), 1.0 / 128); ms(v("ones", 65, 66), -129.0)
     for p in "fb":
-        ms(v("w" + p, 64, 65), 384.0); ms(v("vv" + p, 0, 1), 0.0); ms(v("jr" + p, 0, 1), 0.0)
+        ms(v("w" + p, 64, 66), 384.0); ms(v("vv" + p, 0, 1), 0.0); ms(v("jr" + p, 0, 1), 0.0)
     for p in "fbz":
         ms(v("cb" + p, 144, 160), 1024.0)
     for a in range(16):
-        mul(v("rep", 128 * a, 128 * a + 128), same, col("rc", a))
+        mul(v("rep", 128 * a, 128 * a + 128), same, col("rc", a), BOTH)
     ts(v("par", 0, 4), v("raw", 0, 4), -1.0, A.mult)
-    cp(v("par", 4, 8), v("raw", 1, 5))
+    cp(v("par", 7, 8), v("raw", 7, 8))
+    cp(v("par", 4, 7), v("raw", 4, 7))
     send(prv, v("parF", 0, 8), v("par", 0, 8), "par0", 3.0)
     send(nxt, v("parB", 0, 8), v("par", 0, 8), "par1", 3.0)
+    send(opp, v("parO", 0, 8), v("par", 0, 8), "par2", 3.0)
+    send(prv, v("nzn", 0, S), v("nzs", 0, S), "nzn", 5.0)
     iota(v("itab", 0, 1025), [[1, 1025]], 0, 0)
-    ms(rows("cr", 0, 32, 0, S), 2048.0, 0.5); ms(rows("cr", 96, 128, 3, S), 2048.0, 0.5)
-    iota(rows("cr", 32, 64, 1, S), [[16, 64], [0, 16]], 0, 0)
-    iota(rows("cr", 64, 96, 2, S), [[0, 64], [2, 16]], 1, 0)
+    ms(rows("cr", 0, 64, 0, S), 2048.0, 0.5)
     iota(mat("amr"), [[0, 8], [2, 16]], 1, 0)
+    iota(rows("cr", 64, 96, 1, S), [[16, 64], [0, 16]], 0, 0)
+    iota(rows("cr", 96, 128, 2, S), [[0, 64], [2, 16]], 1, 0)
     mul(rows("cla", 0, 32, 0, 128), (T.amr[0:32, :], ("amr", 0, 128), 128), 1.0 / 32)
     mul(rows("clz", 0, 32, 0, 128), (T.amr[0:32, :], ("amr", 0, 128), 128), 1.0)
-    for nm, lastc in (("cla", 12.0), ("clz", 0.0)):
-        for (p0, c, key) in ((32, 1.0 / 32, 1), (64, 1.0 / 64, 2), (96, lastc, 3)):
-            ms(rows(nm, p0, p0 + 32, key, 64), c)
+    for (nm, p0, c, key) in (("cla", 32, 12.0, 1), ("clz", 32, 0.0, 1), ("clz", 64, 1.0 / 32, 2), ("clz", 96, 1.0 / 64, 3)):
+        ms(rows(nm, p0, p0 + 32, key, 64), c)
     ts(v("thr", 0, 8), v("mrow", 0, 128, 16), ak, A.add, 129.5, A.add)
     ts(v("thr", 8, 16), v("thr", 0, 8), -128.515625, A.add, 32.0, A.mult)
     lin(mat("cq"), mat("mrow"), 1.0, 129.5)
@@ -258,6 +262,7 @@ def build(T, topo, core):
     mul(mat("off"), mat("e0"), -8192.0)
     ts(mat("seg"), mat("amr"), 1.0, A.is_equal, -4096.0, A.mult)
     cp(mat("pio"), mat("pis"))
+    send(prv, mat("pin"), mat("pio"), "pin", 3.0)
     mul(mat("two"), same, 2.0)
     ts(mat("e0"), dm, -2.0, A.mult, ak, A.add)
     lin(mat("e1"), mat("e0"), 1.0, 16.0)
@@ -278,9 +283,9 @@ def build(T, topo, core):
     ts(v("fcn", 0, 129), v("nq", 0, 129), 0.25, A.mult, col("kf", 6), A.add)
 
     def umat(p, ub):
-        cl = "clz" if p == "z" else "cla"
+        cl, k_ = ("clz", 128) if p == "z" else ("cla", 64)
         for h in (0, 1):
-            mms([(bank(ub[h], 0, 512), v(cl, 0, 128, key=(cl, 0, 4)), v("cr", 512 * h, 512 * h + 512, key=("cr", 0, 4)), True, False)])
+            mms([(bank(ub[h], 0, 512), (T[cl][0:k_, :], (cl, 0, 4), 128), (T.cr[0:k_, 512 * h:512 * h + 512], ("cr", 0, 3 if p == "z" else 1), 512), True, False)])
 
     def invert(p, vp, ub, sb, lvl1, thr0):
         V, zz, no, jo = "vv" + vp, "zz" + p, v("no" + p, 0, 8), v("jo" + p, 0, 8)
@@ -323,18 +328,19 @@ def build(T, topo, core):
         umat(p, ub)
         counts(sb, 0, o)
         ts(v("w" + p, 0, 64), bank(sb, 0, 64), 2.0, A.max, 383.75, A.add)
-        mms([(bank(sb, 128, 193), mat("half"), v("c384", 0, 65), True, False), (bank(sb, 128, 193), mat("half"), v("w" + p, 0, 65), False, True),
+        mms([(bank(sb, 128, 194), mat("half"), v("c384", 0, 66), True, False), (bank(sb, 128, 194), mat("half"), v("w" + p, 0, 66), False, True),
              (bank(sb, 200, 264), mat("suf"), v("c384", 0, 64), True, False), (bank(sb, 200, 264), mat("suf"), v("w" + p, 0, 64), False, True)])
         cs = "cs" + p
-        scan(v(cs, 15, 80), v("ones", 0, 65), bank(sb, 128, 193), 0.0, A.mult, A.add)
-        add(["dve"], lambda q, e: q.reciprocal(T["rr" + p][:, 0:1], T[cs][:, 79:80]), 0.25, [(cs, 79, 80)], [("rr" + p, 0, 1)])
+        scan(v(cs, 14, 80), v("ones", 0, 66), bank(sb, 128, 194), 0.0, A.mult, A.add)
+        add(["dve"], lambda q, e: q.reciprocal(T["rr" + p][:, 0:1], T[cs][:, 78:79]), 0.25, [(cs, 78, 79)], [("rr" + p, 0, 1)])
         r = col("rr" + p, 0)
-        tt(v(cs, 80, 144), v(cs, 15, 79), bank(sb, 200, 264), A.subtract, k=1)
-        lin(v("cb" + p, 15, 144), v(cs, 15, 144), r, 128.53125)
-        ts(v("tt" + p, 0, 64), v("cb" + p, 80, 144), -129.0, A.add, col(cs, 79), A.mult)
+        tt(v(cs, 80, 144), v(cs, 14, 78), bank(sb, 200, 264), A.subtract, k=1)
+        lin(v("cb" + p, 80, 144), v(cs, 80, 144), r, 128.53125)
+        lin(v("cb" + p, 14, 78), v(cs, 14, 78), r, 128.53125)
+        lin(v("tt" + p, 0, 64), v("cb" + p, 80, 144), col(cs, 78), col(cs, 79))
         tt(v("rho" + p, 0, 64), v(cs, 80, 144), v("tt" + p, 0, 64), A.subtract)
         lin(v("low" + p, 0, 64), v("rho" + p, 0, 64), r, 12.0 + (0.5 - 2.0 ** -14) / 16)
-        invert(p, p, ub, sb, v("cb" + p, 15, 79), 0)
+        invert(p, p, ub, sb, v("cb" + p, 14, 78), 0)
         cp(mat(lst), mat("aa" + p))
 
     bias[0] = OPT["b0"]
@@ -343,21 +349,23 @@ def build(T, topo, core):
     ancestors("f", "f0s", "par", 0, "lfo0", (0, 1), 7, S)
     for t in range(RO):
         last = t == RO - 1
-        site[0] = 2000 if last else 1000
+        site[0] = 1000 * (t + 1)
         bias[0] = 0.0
-        fw, bw, lf, lb = ("f0s", "b0s", "lfo0", "lbo0") if t == 0 else ("fin%d" % t, "bin%d" % t, "lfi%d" % t, "lbi%d" % t)
+        fw, bw, lf, lb = [("f0s", "b0s", "lfo0", "lbo0"), ("fo0", "bin1", "lfo1", "lbi1"), ("fin2", "bo1", "lfi2", "lbo0"), ("fin3", "bin3", "lfi3", "lbi3")][t]
+        par, nz_, pi_ = ("parF", "nzn", "pin") if t == 1 else ("par", "nzs", "pio")
+        lam, rate = col(par, 4), {"f": col(par, 5), "b": col(par, 6)}
         for c in range(4):
             cp(v("mw", 2 * K + 512 * c, 2 * K + 512 * c + 512), ind(v(bw, 0, S), v(lb, 32 * c, 32 * c + 32)), k=GA, eng=BOTH)
         for c in range(4):
-            cp(v("mw", K + 512 * c, K + 512 * c + 512), ind(v(fw, 0, S), v(lf, 32 * c, 32 * c + 32)), k=GA, eng=BOTH if c == 0 else ("act",))
+            cp(v("mw", K + 512 * c, K + 512 * c + 512), ind(v(fw, 0, S), v(lf, 32 * c, 32 * c + 32)), k=GA, eng=BOTH)
         umat("z", (4, 5))
         for c in range(4):
             lo, hi = 512 * c, 512 * c + 512
             fi = v("mw", K + lo, K + hi)
-            tt(v("dd", lo, hi), ind(v("mw", 2 * K, 3 * K), v("pio", 32 * c, 32 * c + 32)), fi, A.subtract, k=GA)
+            tt(v("dd", lo, hi), ind(v("mw", 2 * K, 3 * K), v(pi_, 32 * c, 32 * c + 32)), fi, A.subtract, k=GA)
             mul(bank(c % 2, 0, 512), v("dd", lo, hi), lam)
             tt(v("mw", lo, hi), fi, bank(c % 2, 0, 512), A.add, k=1)
-            hits("mw", lo, lo, "par", t, c == 3)
+            hits("mw", lo, lo, par, t, c == 3)
             if c % 2:
                 counts(6, 64 * (c // 2), S * (c // 2))
         ts(mat("wz"), bank(6, 0, 128), 8.5, A.is_ge)
@@ -373,57 +381,99 @@ def build(T, topo, core):
         if last:
             for c in range(4):
                 x = v("dd", 512 * c, 512 * c + 512)
-                act(x, x, F.Square)
+                add(list(BOTH), lambda q, e, x=x: q.activation(x[0], x[0], F.Square) if e == "act" else q.tensor_tensor(x[0], x[0], x[0], A.mult),
+                    cost(512, 1.4), rs(x), rs(x))
                 act(x, x, F.Exp, scale=-1.0, extra=1.3 if c == 0 else 0.0)
                 mms([(bank(7, 0, Z), mat("idf"), v("dd", Z * j, Z * j + Z), j == 0, j == 7) for j in (2 * c, 2 * c + 1)], k=4)
             cp(v("yes", 0, Z), bank(7, 0, Z), eng=BOTH)
             dma("sp", T.ye[:], T.yes[:], 2.2, r=[("yes", 0, Z)])
-        for p, sb in (("b", 6), ("f", 2)):
+        first, second = ("f", "b") if t == 1 else ("b", "f")
+        for p, sb in ((first, 6), (second, 2)):
             mms([(bank(sb, 288, 352), mat("p%s0" % p), v("aaz", 0, 128, 2), True, False), (bank(sb, 288, 352), mat("p%s1" % p), v("aaz", 1, 128, 2), False, True)], k=4)
             cp(v("lo" + p, 0, 64), bank(sb, 288, 352))
-        for p, pb in (("b", (0, 1)), ("f", (2, 3))):
+        for p, pb in ((first, (0, 1)), (second, (2, 3))):
             po = "%so%d" % (p, t % 2)
-            bias[0] = OPT["bb"] if p == "b" else 0.0
+            bias[0] = (OPT["bb"] if t == 2 else OPT["bs"]) if p == first else 0.0
             sh = p == "b" and not last
-            dst = prv if p == "b" else nxt
-            for h in (0, 1):
-                lo, hi = 512 * h, 512 * h + 512
-                hv = ind(v("mw", 0, 3 * K if p == "b" else 2 * K), v("lo" + p, 32 * h, 32 * h + 32))
+            dst = (prv if p == "b" else nxt) if t == 2 else opp if p == first else None
+            sc = OPT["scl" if last else "sc"][0 if p == first else 1]
+            for h, (lo, hi) in enumerate(zip(sc, sc[1:])):
+                hv = ind(v("mw", 0, 3 * K if p == "b" else 2 * K), v("lo" + p, lo // 16, hi // 16))
                 x = v("sq" + p, lo, hi)
-                mms([(bank(pb[h], 0, 512), mat("shb" if sh else "idb"), v("nzs", lo, hi), True, False)])
+                bk = bank(pb[h % 2], 0, hi - lo)
+                mms([(bk, mat("shb" if sh else "idb"), v(nz_, lo, hi), True, False)])
                 act(x, hv, F.Square, k=GA)
                 tt(x, hv, x, A.subtract, k=GA)
-                mul(x, x, rate[p])
-                mms([(bank(pb[h], 0, 512), mat("shf" if sh else "idf"), x, False, True)], k=4)
-                ts(v(po, lo, hi), bank(pb[h], 0, 512), 0.0, A.max, 1.0, A.min)
+                mul(x, x, rate[p], BOTH)
+                mms([(bk, mat("shf" if sh else "idf"), x, False, True)], k=4)
+                ts(v(po, lo, hi), bk, 0.0, A.max, 1.0, A.min)
                 if last:
                     dma("sp", T["y" + p][:, lo:hi], T[po][:, lo:hi], 2.4, r=[(po, lo, hi)])
-                else:
-                    send(dst, v("%sin%d" % (p, t + 1), lo, hi), v(po, lo, hi), "%s%s%d" % (p, "ab"[h], t + 1), OPT["tl"] * (1 + h / 4))
+                elif dst is not None and hi % 512 == 0:
+                    send(dst, v("%sin%d" % (p, t + 1), hi - 512, hi), v(po, hi - 512, hi), "%s%s%d" % (p, "ab"[hi // S], t + 1), OPT["tl"] * (1 + hi // S / 4))
             if not last:
                 lst = "l%so%d" % (p, (t + 1) % 2)
-                ancestors(p, po, "parB" if p == "b" else "parF", t + 1, lst, (4, 5) if p == "b" else (0, 1), 6 if p == "b" else 7, 0 if p == "b" else S)
-                send(dst, mat("l%si%d" % (p, t + 1)), mat(lst), "%sl%d" % (p, t + 1), OPT["ll"])
+                ancestors(p, po, {"b": "parB", "f": "parF"}[p] if t != 1 else {"b": "par", "f": "parO"}[p], t + 1, lst,
+                          (4, 5) if p == first else (0, 1), 6 if p == first else 7, 0 if p == first else S)
+                if dst is not None:
+                    send(dst, mat("l%si%d" % (p, t + 1)), mat(lst), "%sl%d" % (p, t + 1), OPT["ll"])
     return ops
 
 
-def schedule(ops):
+def lay(ops, links, key, back, fixed):
     HOP = OPT["hop"]
     n = len(ops)
-    succ = [[] for _ in range(n)]
-    for i, o in enumerate(ops):
-        for j in o["deps"]:
-            succ[j].append(i)
-    prio = [0.0] * n
-    for i in range(n - 1, -1, -1):
-        prio[i] = ops[i]["dur"] + ops[i]["lat"] + max([prio[j] + HOP for j in succ[i]] + [0.0])
-    x = OPT["seed"]
-    for i in range(n):
-        x = (x * 1103515245 + 12345) % 2147483648
-        prio[i] += ops[i]["bias"] + OPT["amp"] * (x / 2147483648.0) + OPT["nudge"].get(ops[i]["site"], 0.0)
+    ins, outs = links[back], links[1 - back]
+    left = [len(x) for x in ins]
+    cand = [i for i in range(n) if not left[i]]
+    busy = {e: [] for e in ("pe", "dve", "act", "pool", "sp")}
+    start, end = [0.0] * n, [0.0] * n
+    while cand:
+        i = min(cand, key=lambda y: key[y])
+        cand.remove(i)
+        o, e = ops[i], fixed[i]
+        r = o["lat"] if back else 0.0
+        for j, kd in ins[i]:
+            a, b = (o, ops[j]) if back else (ops[j], o)
+            free = kd == "model" or (a["kind"] == "c" and b["kind"] == "c" and fixed[j] == e and (kd == "order" or e == "pe"))
+            x = end[j] if free else end[j] + a["lat"] + HOP
+            if x > r:
+                r = x
+        if e is not None:
+            B = busy[e]
+            k = len(B)
+            while k and B[k - 1][1] > r:
+                k -= 1
+            while k < len(B) and B[k][0] < r + o["dur"] - 1e-9:
+                r = max(r, B[k][1])
+                k += 1
+            B.insert(k, (r, r + o["dur"]))
+        start[i], end[i] = r, r + o["dur"]
+        for j, _k in outs[i]:
+            left[j] -= 1
+            if not left[j]:
+                cand.append(j)
+    return start, end, fixed
+
+
+def greedy(ops):
+    HOP = OPT["hop"]
+    n = len(ops)
+    if "succ" not in ops[0]:
+        succ = [[] for _ in range(n)]
+        for i, o in enumerate(ops):
+            for j in o["deps"]:
+                succ[j].append(i)
+        way = [0.0] * n
+        for i in range(n - 1, -1, -1):
+            way[i] = ops[i]["dur"] + ops[i]["lat"] + max([way[j] + HOP for j in succ[i]] + [0.0])
+        ops[0]["succ"], ops[0]["way"] = succ, way
+    succ = ops[0]["succ"]
+    prio = [ops[0]["way"][i] + ops[i]["bias"] + OPT["nudge"].get(ops[i]["site"], 0.0) for i in range(n)]
     left = [len(o["deps"]) for o in ops]
     cand = [i for i in range(n) if left[i] == 0]
     free = {e: 0.0 for e in ("pe", "dve", "act", "pool", "sp")}
+    engs = [[OPT["force"][o["site"]]] if o["site"] in OPT["force"] else o["eng"] for o in ops]
     order = []
     memo = {}
 
@@ -456,10 +506,10 @@ def schedule(ops):
         if arr:
             place(arr[0], None, ready(arr[0], None))
             continue
-        opts = [(max(free[e], ready(i, e)), i, e) for i in cand for e in ops[i]["eng"]]
+        opts = [(max(free[e], ready(i, e)), i, e) for i in cand for e in engs[i]]
         t0, _, e0 = min(opts)
         def rank_(y):
-            return (prio[y[1]] - (OPT["pen"] if len(ops[y[1]]["eng"]) > 1 and y[2] == "dve" else 0.0), -y[1])
+            return (prio[y[1]] - (OPT["pen"] if len(engs[y[1]]) > 1 and y[2] == "dve" else 0.0), -y[1])
         now = [y for y in opts if y[2] == e0 and y[0] <= t0 + 1e-9]
         b = max(now, key=rank_)
         soon = [y for y in opts if y[2] == e0 and t0 + 1e-9 < y[0] < t0 + OPT["look"] * ops[b[1]]["dur"] and rank_(y)[0] > rank_(b)[0] + OPT["margin"]]
@@ -501,25 +551,77 @@ def tune(T, topo, core):
         x[0] = (x[0] * 1103515245 + 12345) % 2147483648
         return seq[(x[0] >> 8) % len(seq)]
 
-    def score(nudge):
-        OPT["nudge"] = nudge
-        order = schedule(ops)
-        on = [o["on"] for o in ops]
+    fsite = sorted({o["site"] for o in ops if len(o["eng"]) > 1})
+
+    def total(order, on):
         return sum(replay(a, order, on, s["hop"]) for a, s in zip(alts, SETS))
+
+    def score(nudge, force):
+        OPT["force"] = force
+        OPT["nudge"] = nudge
+        order = greedy(ops)
+        return total(order, [o["on"] for o in ops])
     cur = {}
-    best = score(cur)
-    for _ in range(OPT["tries"]):
+    frc = {}
+    best = score(cur, frc)
+    for _ in range(OPT["first"]):
         c = dict(cur)
-        for _k in range(pick((1, 2, 4, 8))):
+        for _k in range(pick((1, 2, 3, 5))):
             a, d = pick(range(len(sites))), pick((-3, -1.5, -0.7, -0.3, 0.3, 0.7, 1.5, 3))
             for y in sites[a:a + pick((1, 1, 2, 4, 8))]:
                 c[y] = c.get(y, 0.0) + d
-        s = score(c)
-        if s < best - 0.03:
-            best, cur = s, c
+        f_ = dict(frc)
+        if pick((0, 0, 1)):
+            c = dict(cur)
+            for _k in range(pick((1, 1, 2))):
+                f_[pick(fsite)] = pick(("act", "dve"))
+        s = score(c, f_)
+        if s <= best:
+            best, cur, frc = s, c, f_
     OPT["nudge"] = cur
+    OPT["force"] = frc
+    n = len(ops)
+    ins = [list(o["deps"].items()) for o in ops]
+    outs = [[] for _ in ops]
+    for i in range(n):
+        for j, kd in ins[i]:
+            outs[j].append((i, kd))
+    links = (ins, outs)
+    x[0] = OPT["seed"]
+
+    def rnd():
+        x[0] = (x[0] * 1103515245 + 12345) % 2147483648
+        return x[0] / 2147483648.0
+    order = greedy(ops)
+    on = [o["on"] for o in ops]
+    best = (total(order, on), order, on, [o["start"] for o in ops], [o["end"] for o in ops])
+    flex = [i for i in range(n) if len(ops[i]["eng"]) > 1]
+    for it in range(OPT["tries"]):
+        on, key = list(best[2]), best[3]
+        t0, amp, u = rnd() * max(key), OPT["amp"] * rnd(), rnd()
+        if u < 0.4:
+            i = flex[int(rnd() * len(flex))]
+            on[i] = "act" if on[i] == "dve" else "dve"
+        if u > 0.3:
+            key = [y + (amp * rnd() if t0 < y < t0 + OPT["span"] else 0.0) for y in key]
+        if rnd() < OPT["back"]:
+            _s, back, _o = lay(ops, links, [-y for y in key], 1, on)
+            key = [-y for y in back]
+        st, en, on = lay(ops, links, key, 0, on)
+        order = sorted(range(n), key=lambda i: (st[i], i))
+        sc = total(order, on)
+        if sc <= best[0]:
+            best = (sc, order, on, st, en)
+    OPT["plan"] = best
     OPT["tries"] = 0
-    OPT["best"] = best / len(SETS)
+    OPT["best"] = best[0] / len(SETS)
+
+
+def schedule(ops):
+    _, order, on, st, en = OPT["plan"]
+    for i, o in enumerate(ops):
+        o["on"] = on[i]; o["start"] = st[i]; o["end"] = en[i]; o["done"] = en[i] + o["lat"]
+    return order
 
 
 def rank_program(g, core, T, topo):

@@ -1,8 +1,10 @@
+from concourse.bass import DstId, RemoteDMATransfer
 from concourse.mybir import AluOpType, ActivationFunctionType
 
 A = AluOpType
 F = ActivationFunctionType
 S, K, RO, Z = 1024, 2048, 4, 256
+GAP = 32.5 / 128
 f32, b16, u16, i32 = "float32", "bfloat16", "uint16", "int32"
 
 SCRATCH = {}
@@ -14,44 +16,50 @@ def _sb(name, n, d=f32):
 
 for _n in ("f0s", "b0s", "nzs"):
     _sb(_n, S, b16)
-for _n in ("b%s1", "f%s2", "f%s3", "b%s3"):
+for _n in ("f%s1", "f%s2", "f%s3", "b%s3"):
     _sb(_n % "in", S); _sb("l" + _n % "i", 128, u16)
 for _t in (0, 1):
     _sb("fo%d" % _t, S); _sb("bo%d" % _t, S)
     _sb("lfo%d" % _t, 128, u16); _sb("lbo%d" % _t, 128, u16)
-_sb("raw", 8); _sb("par", 8); _sb("parF", 8); _sb("parB", 8); _sb("parO", 8); _sb("nzn", S, b16); _sb("pin", 128, u16); _sb("pis", 128, i32); _sb("pio", 128, u16)
-_sb("mw", 3 * K); _sb("dd", K); _sb("ab", K); _sb("hh", K, b16); _sb("yes", Z)
+_sb("neg", 4); _sb("par", 8); _sb("parF", 8); _sb("parB", 8); _sb("parO", 8)
+_sb("nzB", S, b16); _sb("nzO", S, b16); _sb("piB", 128, u16); _sb("piO", 128, u16); _sb("pis", 128, i32); _sb("pio", 128, u16)
+_sb("mw", 2 * K); _sb("fi", K); _sb("ba", K); _sb("tb", K); _sb("sm", K); _sb("dd", K); _sb("ab", K); _sb("hh", K, b16)
+_sb("lfl", 128); _sb("lbl", 128); _sb("yes", Z)
 for _p in "fbz":
-    _sb("w" + _p, 128, b16); _sb("cs" + _p, 144); _sb("cb" + _p, 160, b16); _sb("tt" + _p, 64)
-    _sb("low" + _p, 64, b16); _sb("na" + _p, 8); _sb("no" + _p, 8, u16); _sb("zz" + _p, 256, b16); _sb("jo" + _p, 8, u16)
-    _sb("jr" + _p, 136); _sb("aa" + _p, 128)
+    _sb("w" + _p, 136, b16); _sb("cs" + _p, 144); _sb("cb" + _p, 160, b16); _sb("tt" + _p, 64)
+    _sb("low" + _p, 128, b16); _sb("na" + _p, 8); _sb("no" + _p, 8, u16); _sb("zz" + _p, 256, b16); _sb("jo" + _p, 8, u16)
+    _sb("jr" + _p, 136); _sb("aa" + _p, 128); _sb("js" + _p, 128)
 for _p in "fb":
     _sb("sq" + _p, S); _sb("vv" + _p, 1032); _sb("lo" + _p, 64, u16); _sb("rr" + _p, 4); _sb("rho" + _p, 64)
-_sb("junk", 512, b16); _sb("fbk", 132); _sb("nq", 132); _sb("fcn", 132); _sb("js", 128); _sb("seg", 128)
-_sb("sel", 144, b16); _sb("rep", 2048, b16); _sb("itab", 1032); _sb("cr", S, b16); _sb("cla", 128, b16); _sb("clz", 128, b16)
-_sb("ki", 4, i32); _sb("kf", 8); _sb("mrow", 144); _sb("dm", 128, b16); _sb("tmp", 128, b16); _sb("tm2", 128, b16); _sb("same", 128, b16)
-_sb("rc", 16); _sb("amr", 128); _sb("thr", 16); _sb("cq", 128); _sb("ones", 72); _sb("c384", 72, b16); _sb("e0", 128); _sb("e1", 128)
-for _n in ("half", "suf", "two", "me", "mo", "idb", "shb", "off"):
-    _sb(_n, 128, b16)
-for _n in ("pf0", "pf1", "pb0", "pb1", "idf", "shf"):
-    _sb(_n, 128)
+_sb("junk", 1536, b16); _sb("fbk", 128); _sb("nq", 128); _sb("fcn", 128); _sb("seg", 128)
+_sb("sel", 144, b16); _sb("rep", 2048, b16); _sb("rep8", 1024, b16); _sb("rc8", 8); _sb("hm", 4); _sb("itab", 1032)
+_sb("cr", S, b16); _sb("cla", 128, b16); _sb("clz", 128, b16)
+_sb("ki", 4, i32); _sb("kf", 12); _sb("mrow", 144); _sb("dm", 128, b16); _sb("tmp", 128, b16); _sb("tm2", 128, b16); _sb("same", 128, b16)
+_sb("amr", 128); _sb("thr", 16); _sb("cq", 128); _sb("ones", 72); _sb("c384", 136, b16); _sb("e0", 128); _sb("e1", 128)
+PACK = {}
+for _b, _d, _names in (("cm", b16, ("half", "suf", "two", "me", "mo", "ne", "no", "idb", "idn", "shb")),
+                       ("cf", f32, ("pf0", "pf1", "pb0", "pb1", "idf", "shf", "evn", "odd"))):
+    _sb(_b, 128 * len(_names), _d)
+    PACK.update({_n: (_b, 128 * _k) for _k, _n in enumerate(_names)})
 for _k in range(8):
     SCRATCH["bk%d" % _k] = ("psum", [128, 512], f32)
 
-NDMA = 48
-ARR = ["par0", "par1", "par2", "nzn", "pin"] + [n % k for n in ("b%s1", "f%s2", "f%s3", "b%s3") for k in "abl"]
+NDMA = 40
+ARR = ["par", "nzB", "piB", "nzO", "piO"] + [n % k for n in ("f%s1", "f%s2", "f%s3", "b%s3") for k in "abl"]
 SEMAPHORES = ["pe", "dve", "act", "pool"] + ["d%d" % k for k in range(NDMA)] + ARR
 
-OPT = {"cy": 0.00083, "pec": 0.00042, "hop": 0.2, "fix": 0.02, "ga": 1.56, "tl": 4.0, "ll": 2.0,
-       "pen": 3.0, "first": 380, "span": 5.0, "back": 0.5, "look": 0.3, "margin": 0.2, "bb": 2.0, "bs": 3.0, "b0": 3.0, "seed": 0, "amp": 2.5,
-       "nudge": {}, "force": {}, "tries": 3000, "cuts": (0, 512, 1024, 1536, 2048),
-       "sc": ((0, 256, 512, 1024), (0, 512, 1024)), "scl": ((0, 512, 1024), (0, 512, 768, 1024))}
-SETS = [{"cy": 0.00083, "hop": 0.2, "fix": 0.02, "pec": 0.00042, "ll": 2.0, "ga": 1.56},
-        {"cy": 0.0012, "hop": 0.22, "fix": 0.03, "pec": 0.0006, "ll": 3.0, "tl": 6.0, "ga": 2.0}]
+OPT = {"padd": (1, 0, 0, 0), "yb": (0, 1), "early": ((0, "b"), (1, "b"), (2, "b"), (3, "b")), "ysq": (), "zs": (0, 1), "lb_": ((7, 2), (7, 2), (7, 2), (7, 2)), "dadd": [(t, "f", h) for t in range(4) for h in range(4)] + [(3, "b", 0), (3, "b", 1)],
+       "pb": ((0, 1, 2, 3), (4, 5)), "ub": ((0, 1), (2, 3)), "bb_": (4, 5), "hc": ((0, 256, 512, 768, 1024), (0, 512, 1024)),
+       "sc": ((0, 256, 512, 768, 1024), (0, 512, 1024)), "scl": ((0, 512, 1024), (0, 512, 768, 1024)),
+       "tries": 250, "inner": 200, "width": 150, "temp": 0.3, "slack": 0.0, "seed": 1}
+SETS = [{"cy": 0.00083, "hop": 0.2, "fix": 0.02, "pec": 0.00042, "ll": 2.0, "tl": 4.0, "ga": 1.56, "wt": 1.0},
+        {"cy": 0.00083, "hop": 0.2, "fix": 0.02, "pec": 0.00084, "ll": 2.0, "tl": 4.0, "ga": 1.3, "wt": 0.8},
+        {"cy": 0.0011, "hop": 0.24, "fix": 0.03, "pec": 0.0006, "ll": 4.0, "tl": 8.0, "ga": 1.9, "wt": 0.4}]
+QUEUES = ("pe", "dve", "act", "pool", "sp")
 
 
-def build(T, topo, core):
-    CY, PEC, GA = OPT["cy"], OPT["pec"], OPT["ga"]
+def build(T, topo, core, tm):
+    CY, PEC, GA = tm["cy"], tm["pec"], tm["ga"]
     rank = T.rank_of(core)
     n = len(T.cores)
     nxt, prv = T.cores[(rank + 1) % n], T.cores[(rank - 1) % n]
@@ -59,7 +67,6 @@ def build(T, topo, core):
     ops = []
     hist = {}
     lastbank = {}
-    bias = [0.0]
     site = [0]
     BOTH = ("act", "dve")
 
@@ -79,14 +86,16 @@ def build(T, topo, core):
                     if j is not None and j != i and j not in deps:
                         deps[j] = "order"
                     lastbank[nm] = i
+                if isw:
+                    h[:] = [y for y in h if not (lo <= y[1] and y[2] <= hi)]
                 h.append((i, lo, hi, isw))
         ops.append({"eng": eng, "fn": fn, "dur": dur, "deps": deps, "kind": kind, "lat": lat, "sem": sem, "cnt": cnt,
-                    "bias": bias[0], "tag": (list(w) + list(r))[0], "site": site[0]})
-        site[0] += 1
+                    "tag": (list(w) + list(r))[0], "site": site[0]})
         return i
 
     def v(nm, lo, hi, step=1, key=None):
-        ap_ = T[nm][:, lo:hi] if step == 1 else T[nm][:, lo:hi:step]
+        buf, o = PACK.get(nm, (nm, 0))
+        ap_ = T[buf][:, o + lo:o + hi] if step == 1 else T[buf][:, o + lo:o + hi:step]
         return (ap_, (nm, lo, hi) if key is None else key, len(range(lo, hi, step)))
 
     def ind(win, off):
@@ -105,7 +114,7 @@ def build(T, topo, core):
         return x[0] if isinstance(x, tuple) else x
 
     def cost(n_, k=1.0):
-        return OPT["fix"] + max(64, n_ * k) * CY
+        return tm["fix"] + max(64, n_ * k) * CY + (0.035 if k == GA else 0.0)
 
     def ts(out, in0, s1, op0, s2=None, op1=None, k=1.0):
         def fn(q, e):
@@ -124,12 +133,12 @@ def build(T, topo, core):
             return q.activation(out[0], in_[0], F.Copy)
         return add(list(eng), fn, cost(in_[2], k), rs(in_), rs(out))
 
-    def mul(out, in_, c, eng=("act",)):
+    def mul(out, in_, c, eng=("act",), k=1.0):
         def fn(q, e):
             if e == "dve":
                 return q.tensor_scalar(out[0], in_[0], ap(c), None, A.mult)
             return q.activation(out[0], in_[0], F.Identity, scale=ap(c))
-        return add(list(eng), fn, cost(in_[2]), rs(in_, c), rs(out))
+        return add(list(eng), fn, cost(in_[2], k), rs(in_, c), rs(out))
 
     def lin(out, in_, scale, bias_):
         def fn(q, e):
@@ -161,7 +170,7 @@ def build(T, topo, core):
             if integer:
                 return q.iota(out[0], pat, base, cm)
             return q.iota(out[0], pat, base, cm, allow_small_or_imprecise_dtypes=True)
-        return add(["pool"], fn, 0.13 + 2 * CY * out[2], [("poolq", 0, 1)], rs(out) + [("poolq", 0, 1)])
+        return add(["pool"], fn, 0.13 + 2 * CY * out[2], [], rs(out) + [("poolq", 0, 1)])
 
     nd = [0]
 
@@ -185,7 +194,7 @@ def build(T, topo, core):
         m = sum(1 << e for e in es)
         ls = dsem()
         i = add(["pool"], lambda q, e: q.remote_dma(out[0], in_[0], T.sem[rsem], T.sem[ls], pid, rid, m), 0.5, rs(in_), [],
-                kind="dma", lat=lat, sem=ls, cnt=len(es))
+                kind="far", lat=lat, sem=ls, cnt=len(es))
         add([None], None, 0.0, [], rs(out), kind="arr", lat=lat, sem=rsem, cnt=len(narrow), after=[i])
 
     def bank(k_, lo, hi, step=1):
@@ -201,13 +210,13 @@ def build(T, topo, core):
         return (T[nm][p0:p1, :], (nm, key, key + 1), width)
 
     dma("sp", T.b0s[:], T.b0[:], 2.6, w=[("b0s", 0, S)])
-    dma("act", T.raw[:, 0:4], T.obs[:], 2.0, w=[("raw", 0, 4)])
-    dma("act", T.raw[:, 7:8], T.eps[:], 2.0, w=[("raw", 7, 8)])
+    dma("act", T.par[:, 0:4], T.obs[:], 2.0, w=[("par", 0, 4)])
+    dma("act", T.par[:, 7:8], T.eps[:], 2.0, w=[("par", 7, 8)])
     dma("sp", T.f0s[:], T.f0[:], 3.0, w=[("f0s", 0, S)])
     dma("sp", T.pis[:], T.pi[:], 3.0, w=[("pis", 0, 128)])
-    dma("sp", T.raw[:, 4:5], T.lam[:], 3.0, w=[("raw", 4, 5)])
-    dma("sp", T.raw[:, 5:6], T.rf[:], 3.0, w=[("raw", 5, 6)])
-    dma("sp", T.raw[:, 6:7], T.rb[:], 3.0, w=[("raw", 6, 7)])
+    dma("sp", T.par[:, 4:5], T.lam[:], 3.0, w=[("par", 4, 5)])
+    dma("sp", T.par[:, 5:6], T.rf[:], 3.0, w=[("par", 5, 6)])
+    dma("sp", T.par[:, 6:7], T.rb[:], 3.0, w=[("par", 6, 7)])
     dma("sp", T.nzs[:], T.nz[:], 3.0, w=[("nzs", 0, S)])
 
     iota(v("ki", 0, 1), [[0, 1]], 0, 1, integer=True)
@@ -216,71 +225,87 @@ def build(T, topo, core):
     cp(v("kf", 0, 2), v("ki", 0, 2))
     kk, ak = col("kf", 0), col("kf", 1)
     tt(col("kf", 2), kk, ak, A.subtract)
-    bias[0] = 20.0
     ts(mat("dm"), mat("mrow"), col("kf", 2), A.subtract)
     dm = mat("dm")
     ts(mat("tmp"), dm, -0.5, A.is_gt, k=0.5)
     ts(mat("tm2"), dm, 15.5, A.is_lt, k=0.5)
     tt(mat("same"), mat("tmp"), mat("tm2"), A.mult, k=1)
     same = mat("same")
-    ts(v("rc", 0, 16), v("mrow", 0, 16), ak, A.is_equal, -65536.0, A.mult)
-    bias[0] = 0.0
     ts(v("sel", 0, 144), v("mrow", 0, 144), col("kf", 2), A.subtract, 15.0, A.is_equal)
-    mul(mat("half"), same, 0.5)
+    mul(mat("half"), same, 0.5, BOTH)
     ts(mat("tmp"), dm, ak, A.is_lt, 0.5, A.mult, k=0.5)
     tt(mat("suf"), mat("tmp"), same, A.mult, k=1)
-    ms(v("c384", 0, 72), -384.0); ms(v("ones", 0, 64), 1.0); ms(v("ones", 64, 65), 1.0 / 128); ms(v("ones", 65, 66), -129.0)
+    ms(v("c384", 0, 64), -384.0); ms(v("c384", 64, 65), 0.0); ms(v("c384", 65, 66), GAP / 8); ms(v("c384", 72, 136), -GAP)
+    ms(v("ones", 0, 64), 1.0); ms(v("ones", 64, 65), 1.0 / 128); ms(v("ones", 65, 66), -129.0)
     for p in "fb":
-        ms(v("w" + p, 64, 66), 384.0); ms(v("vv" + p, 0, 1), 0.0); ms(v("jr" + p, 0, 1), 0.0)
+        ms(v("w" + p, 64, 66), 0.0); ms(v("vv" + p, 0, 1), 0.0)
     for p in "fbz":
-        ms(v("cb" + p, 144, 160), 1024.0)
-    for a in range(16):
-        mul(v("rep", 128 * a, 128 * a + 128), same, col("rc", a), BOTH)
-    ts(v("par", 0, 4), v("raw", 0, 4), -1.0, A.mult)
-    cp(v("par", 7, 8), v("raw", 7, 8))
-    cp(v("par", 4, 7), v("raw", 4, 7))
-    send(prv, v("parF", 0, 8), v("par", 0, 8), "par0", 3.0)
-    send(nxt, v("parB", 0, 8), v("par", 0, 8), "par1", 3.0)
-    send(opp, v("parO", 0, 8), v("par", 0, 8), "par2", 3.0)
-    send(prv, v("nzn", 0, S), v("nzs", 0, S), "nzn", 5.0)
-    iota(v("itab", 0, 1025), [[1, 1025]], 0, 0)
-    ms(rows("cr", 0, 64, 0, S), 2048.0, 0.5)
+        ms(v("jr" + p, 0, 1), 0.0)
+    act(v("cbb", 144, 160), v("ones", 0, 16), F.Exp, scale=7.0, extra=1.3)
+    for p in "fz":
+        cp(v("cb" + p, 144, 160), v("cbb", 144, 160), eng=BOTH)
+    ts(col("hm", 0), ak, 7.5, A.is_lt); ts(col("hm", 1), ak, 7.5, A.is_gt)
+    ts(v("hm", 2, 4), v("hm", 0, 2), 12.0 + (0.5 - 2.0 ** -14) / 16, A.mult)
+    ts(col("kf", 7), col("hm", 1), -8.0, A.mult, ak, A.add)
+    ts(v("rc8", 0, 8), v("mrow", 0, 8), col("kf", 7), A.is_equal, -65536.0, A.mult)
+    for a in range(8):
+        mul(v("rep8", 128 * a, 128 * a + 128), same, col("rc8", a), BOTH)
+    ms(v("wz", 0, 2), 0.0)
+    ts(col("neg", 2), col("par", 0), -1.0, A.mult)
+    ts(v("neg", 0, 2), v("par", 5, 7), -1.0, A.mult)
     iota(mat("amr"), [[0, 8], [2, 16]], 1, 0)
+    iota(rows("cr", 0, 64, 0, S), [[0, S]], 2048, 0)
+    iota(v("itab", 0, 1025), [[1, 1025]], 0, 0)
     iota(rows("cr", 64, 96, 1, S), [[16, 64], [0, 16]], 0, 0)
     iota(rows("cr", 96, 128, 2, S), [[0, 64], [2, 16]], 1, 0)
-    mul(rows("cla", 0, 32, 0, 128), (T.amr[0:32, :], ("amr", 0, 128), 128), 1.0 / 32)
-    mul(rows("clz", 0, 32, 0, 128), (T.amr[0:32, :], ("amr", 0, 128), 128), 1.0)
-    for (nm, p0, c, key) in (("cla", 32, 12.0, 1), ("clz", 32, 0.0, 1), ("clz", 64, 1.0 / 32, 2), ("clz", 96, 1.0 / 64, 3)):
+    mul(rows("cla", 0, 32, 0, 128), (T.amr[0:32, :], ("amr", 0, 128), 128), 1.0 / 32, BOTH)
+    mul(rows("clz", 0, 32, 0, 128), (T.amr[0:32, :], ("amr", 0, 128), 128), 1.0, BOTH)
+    for (nm, p0, c, key) in (("cla", 32, 12.0, 1), ("clz", 32, -15.5, 1), ("clz", 64, 1.0 / 32, 2), ("clz", 96, 1.0 / 64, 3)):
         ms(rows(nm, p0, p0 + 32, key, 64), c)
-    ts(v("thr", 0, 8), v("mrow", 0, 128, 16), ak, A.add, 129.5, A.add)
-    ts(v("thr", 8, 16), v("thr", 0, 8), -128.515625, A.add, 32.0, A.mult)
+    ts(v("thr", 0, 8), v("mrow", 0, 128, 16), ak, A.add, 1.0, A.add)
+    lin(v("thr", 8, 16), v("thr", 0, 8), 32.0, -0.5)
     lin(mat("cq"), mat("mrow"), 1.0, 129.5)
     ts(mat("idf"), dm, ak, A.is_equal)
-    mul(mat("idb"), mat("idf"), 1.0)
+    mul(mat("idb"), mat("idf"), 1.0, BOTH)
     ts(col("kf", 4), ak, 2.0, A.mult)
-    ts(mat("e0"), mat("amr"), col("kf", 4), A.subtract, 1.0, A.not_equal)
-    mul(mat("off"), mat("e0"), -8192.0)
-    ts(mat("seg"), mat("amr"), 1.0, A.is_equal, -4096.0, A.mult)
+    ts(mat("e0"), mat("amr"), col("kf", 4), A.subtract, 1.0, A.is_equal)
+    mul(mat("seg"), mat("e0"), 4096.0, BOTH)
     cp(mat("pio"), mat("pis"))
-    send(prv, mat("pin"), mat("pio"), "pin", 3.0)
-    mul(mat("two"), same, 2.0)
+    ways = {}
+    for dst, to in ((prv, "parF"), (nxt, "parB"), (opp, "parO")):
+        ways.setdefault(sum(1 << e for e in emask[dst]), []).append((topo.addr(dst, core), to))
+    ls = dsem()
+    i = add(["pool"], lambda q, e: q.remote_dma_fused([
+        RemoteDMATransfer(dst_ids=[DstId(rid=a[0], pnc=a[1]) for a, to in ds], dma_engine_mask=m, remote_sem=T.sem["par"], srcs=[T.par[:]], dsts=[T[to][:] for a, to in ds])
+        for m, ds in ways.items()], local_sem=T.sem[ls]), 1.0, [("par", 0, 8), ("poolq", 0, 1)], [], kind="far", lat=6.0, sem=ls, cnt=len(narrow) * len(ways))
+    add([None], None, 0.0, [], [(to, 0, 8) for to in ("parF", "parB", "parO")], kind="arr", lat=6.0, sem="par", cnt=3 * len(narrow), after=[i])
+    for to, frm, w_ in (("nzB", "nzs", S), ("piB", "pio", 128)):
+        send(nxt, v(to, 0, w_), v(frm, 0, w_, key=[(frm, 0, w_), ("poolq", 0, 1)]), to, 12.0)
+    for h in (0, 1):
+        mul(v("rep", S * h, S * h + S), v("rep8", 0, S), col("hm", h), ("dve",), k=0.5)
+    mul(mat("two"), same, 2.0, BOTH)
     ts(mat("e0"), dm, -2.0, A.mult, ak, A.add)
     lin(mat("e1"), mat("e0"), 1.0, 16.0)
     for nm, e_, t_ in (("me", "e0", "tmp"), ("mo", "e1", "tm2")):
         ts(mat(t_), mat(e_), 0.0, A.max, 2.0, A.min)
         tt(mat(nm), mat(t_), same, A.mult, k=1)
+        tt(mat("n" + nm[1]), mat("two"), mat(nm), A.subtract, k=1)
     for nm, e_, c in (("pf0", "e0", 0.0), ("pf1", "e1", 0.0), ("pb0", "e0", 1.0), ("pb1", "e1", 1.0)):
         ts(mat(nm), mat(e_), c, A.is_equal, 2.0, A.mult)
     ts(col("ki", 2), col("ki", 0), 16.0, A.add)
     ts(col("ki", 3), col("ki", 2), 127, A.bitwise_and)
     cp(col("kf", 3), col("ki", 3))
     ts(mat("shf"), mat("mrow"), col("kf", 3), A.is_equal)
-    mul(mat("shb"), mat("shf"), 1.0)
-    ts(v("nq", 0, 129), v("mrow", 0, 129), 32.0, A.mult, col("kf", 4), A.add)
+    mul(mat("shb"), mat("shf"), -1.0, BOTH)
+    mul(mat("idn"), mat("idf"), -1.0, BOTH)
+    lin(mat("nq"), mat("mrow"), 32.0, col("kf", 4))
     ts(col("ki", 2), col("ki", 0), 1, A.bitwise_and)
     cp(col("kf", 5), col("ki", 2))
-    ts(col("kf", 6), col("kf", 5), 1023.5, A.mult, 1024.0, A.add)
-    ts(v("fcn", 0, 129), v("nq", 0, 129), 0.25, A.mult, col("kf", 6), A.add)
+    ts(col("kf", 6), col("kf", 5), 512.0, A.mult)
+    ts(col("kf", 8), col("kf", 5), -0.5, A.mult, 0.5, A.add)
+    ts(col("kf", 9), ak, 1.0, A.add)
+    mul(mat("evn"), mat("idf"), col("kf", 8), BOTH)
+    ts(mat("odd"), dm, col("kf", 9), A.is_equal, col("kf", 8), A.mult)
 
     def umat(p, ub):
         cl, k_ = ("clz", 128) if p == "z" else ("cla", 64)
@@ -288,369 +313,367 @@ def build(T, topo, core):
             mms([(bank(ub[h], 0, 512), (T[cl][0:k_, :], (cl, 0, 4), 128), (T.cr[0:k_, 512 * h:512 * h + 512], ("cr", 0, 3 if p == "z" else 1), 512), True, False)])
 
     def invert(p, vp, ub, sb, lvl1, thr0):
-        V, zz, no, jo = "vv" + vp, "zz" + p, v("no" + p, 0, 8), v("jo" + p, 0, 8)
+        V, zz, no, jo, jk = "vv" + vp, "zz" + p, v("no" + p, 0, 8), v("jo" + p, 0, 8), 512 * "fbz".index(p)
         for cc in range(8):
-            act(v("junk", 64 * cc, 64 * cc + 64), lvl1, F.Sign, bias=col("thr", thr0 + cc), scale=-1.0, acc=col("na" + p, cc))
+            act(v("junk", jk + 64 * cc, jk + 64 * cc + 64), lvl1, F.Sign, bias=col(thr0[0], thr0[1] + cc), scale=-1.0, acc=col("na" + p, cc), extra=0.02)
         ts(no, v("na" + p, 0, 8), 0.5, A.mult, 32.0, A.add)
         tt(v(zz, 0, 128), ind(v("cb" + p, 80, 160), no), mat("cq"), A.is_lt, k=GA)
-        cp(v(zz, 128, 256), ind(v("itab", 0, 72), no), k=GA, eng=("act",))
+        cp(v(zz, 128, 256), ind(v("itab", 0, 72), no), k=GA, eng=BOTH)
         for h in (0, 1):
-            mms([(bank(ub[h], a, 512, 16), v("rep", 128 * a, 128 * a + 128), v("low" + p, 32 * h, 32 * h + 32), False, a == 15) for a in range(16)])
-        mms([(bank(sb, 0, 128), mat("idb"), mat("off"), True, False), (bank(sb, 0, 128), same, v(zz, 128, 256), False, False), (bank(sb, 0, 128), same, v(zz, 0, 128), False, True),
-             (bank(sb, 128, 256), same, v(zz, 128, 256), True, False), (bank(sb, 128, 256), same, v(zz, 0, 128), False, True)])
-        scan(mat("js"), mat("seg"), bank(sb, 0, 128), 0.0, A.add, A.max)
-        cp(jo, v("js", 15, 128, 16))
-        if p == "z":
-            ts(v("fbk", 0, 129), v("nq", 0, 129), col("csz", 127), A.is_ge)
-            tt(v("jrz", 0, 129), v("fbk", 0, 129), v("fcn", 0, 129), A.mult)
-            tt(v("jrz", 1, 129), v("jrz", 1, 129), bank(sb, 128, 256), A.max, k=1)
-        else:
-            cp(v("jr" + p, 1, 129), bank(sb, 128, 256), eng=BOTH)
+            if p == "z":
+                mms([(bank(ub[h], a, 512, 16), v("rep", 128 * a, 128 * a + 128), v("low" + p, 32 * h, 32 * h + 32), False, a == 15) for a in range(16)])
+            else:
+                both = [("low%s%d" % (p, e), 0, 128) for e in (0, 1)]
+                mms([(bank(ub[h], a, 512, 8), v("rep8", 128 * a, 128 * a + 128), v("low" + p, 64 * h, 64 * h + 64, key=both), False, a == 7) for a in range(8)])
+        mms([(bank(sb, 0, 128), same, v(zz, 128, 256), True, False), (bank(sb, 0, 128), same, v(zz, 0, 128), False, True)])
+        scan(mat("js" + p), mat("seg"), bank(sb, 0, 128), 0.0, A.add, A.min)
+        cp(jo, v("js" + p, 15, 128, 16))
+        cp(v("jr" + p, 1, 129), bank(sb, 0, 128), eng=BOTH)
         for h in (0, 1):
             scan(v(V, 1 + 512 * h, 513 + 512 * h), bank(ub[h], 0, 512), v("itab", 1 + 512 * h, 513 + 512 * h), col(V, 512 * h), A.max, A.min)
         tt(mat("aa" + p), ind(v(V, 0, 1025), jo), v("jr" + p, 0, 128), A.max, k=GA)
 
-    def hits(x, xo, o, prm, t, split):
+    def hits(x, xo, o, prm, t, split, w=512):
         for e in ((0, 1) if split else (None,)):
             st, d = (1, 0) if e is None else (2, e)
-            keys = [[(nm + s_, o, o + 512) for s_ in ("01" if e is None else str(e))] for nm in ("ab", "hh")]
-            a_ = v("ab", o + d, o + 512, st, key=keys[0])
-            act(a_, v(x, xo + d, xo + 512, st), F.Abs, bias=col(prm, t))
-            ts(v("hh", o + d, o + 512, st, key=keys[1]), a_, col(prm, 7), A.is_le)
+            keys = [[(nm + s_, o, o + w) for s_ in ("01" if e is None else str(e))] for nm in ("ab", "hh")]
+            a_ = v("ab", o + d, o + w, st, key=keys[0])
+            act(a_, v(x, xo + d, xo + w, st), F.Abs, bias=col(prm, t) if t else col("neg", 2))
+            ts(v("hh", o + d, o + w, st, key=keys[1]), a_, col(prm, 7), A.is_le)
 
     def counts(sb, c0, o):
         for e in (0, 1):
             mms([(bank(sb, c0, c0 + 64), v("sel", 15 - a, 143 - a), v("hh", o + a, o + S, 16, key=("hh%d" % e, o, o + S)), a == 0, a == 15) for a in range(e, 16, 2)])
 
-    def ancestors(p, x, prm, t, lst, ub, sb, o):
-        hits(x, 0, o, prm, t, False)
-        hits(x, 512, o + 512, prm, t, True)
+    def ancestors(p, x, prm, t, lst, ub, sb, o, hc=(0, 512, 1024)):
+        for lo, hi in zip(hc, hc[1:]):
+            hits(x, lo, o + lo, prm, t, hi == S, hi - lo)
         umat(p, ub)
         counts(sb, 0, o)
         ts(v("w" + p, 0, 64), bank(sb, 0, 64), 2.0, A.max, 383.75, A.add)
         mms([(bank(sb, 128, 194), mat("half"), v("c384", 0, 66), True, False), (bank(sb, 128, 194), mat("half"), v("w" + p, 0, 66), False, True),
-             (bank(sb, 200, 264), mat("suf"), v("c384", 0, 64), True, False), (bank(sb, 200, 264), mat("suf"), v("w" + p, 0, 64), False, True)])
+             (bank(sb, 200, 264), mat("suf"), v("c384", 0, 64), True, False), (bank(sb, 200, 264), mat("idb"), v("c384", 72, 136), False, False),
+             (bank(sb, 200, 264), mat("suf"), v("w" + p, 0, 64), False, True)])
         cs = "cs" + p
         scan(v(cs, 14, 80), v("ones", 0, 66), bank(sb, 128, 194), 0.0, A.mult, A.add)
         add(["dve"], lambda q, e: q.reciprocal(T["rr" + p][:, 0:1], T[cs][:, 78:79]), 0.25, [(cs, 78, 79)], [("rr" + p, 0, 1)])
         r = col("rr" + p, 0)
         tt(v(cs, 80, 144), v(cs, 14, 78), bank(sb, 200, 264), A.subtract, k=1)
-        lin(v("cb" + p, 80, 144), v(cs, 80, 144), r, 128.53125)
-        lin(v("cb" + p, 14, 78), v(cs, 14, 78), r, 128.53125)
+        lin(v(cs, 0, 8), v("thr", 0, 8), col(cs, 78), -GAP)
+        lin(v("cb" + p, 80, 144), v(cs, 80, 144), r, 128.5)
         lin(v("tt" + p, 0, 64), v("cb" + p, 80, 144), col(cs, 78), col(cs, 79))
         tt(v("rho" + p, 0, 64), v(cs, 80, 144), v("tt" + p, 0, 64), A.subtract)
-        lin(v("low" + p, 0, 64), v("rho" + p, 0, 64), r, 12.0 + (0.5 - 2.0 ** -14) / 16)
-        invert(p, p, ub, sb, v("cb" + p, 14, 78), 0)
+        mul(v("rr" + p, 2, 4), v("hm", 0, 2), r, BOTH)
+        for e in (0, 1):
+            lin(v("low" + p, e, 128, 2, key=("low%s%d" % (p, e), 0, 128)), v("rho" + p, 0, 64), col("rr" + p, 2 + e), col("hm", 2 + e))
+        invert(p, p, ub, sb, v(cs, 14, 78), (cs, 0))
         cp(mat(lst), mat("aa" + p))
 
-    bias[0] = OPT["b0"]
     ancestors("b", "b0s", "par", 0, "lbo0", (4, 5), 6, 0)
-    bias[0] = 0.0
     ancestors("f", "f0s", "par", 0, "lfo0", (0, 1), 7, S)
     for t in range(RO):
         last = t == RO - 1
-        site[0] = 1000 * (t + 1)
-        bias[0] = 0.0
-        fw, bw, lf, lb = [("f0s", "b0s", "lfo0", "lbo0"), ("fo0", "bin1", "lfo1", "lbi1"), ("fin2", "bo1", "lfi2", "lbo0"), ("fin3", "bin3", "lfi3", "lbi3")][t]
-        par, nz_, pi_ = ("parF", "nzn", "pin") if t == 1 else ("par", "nzs", "pio")
-        lam, rate = col(par, 4), {"f": col(par, 5), "b": col(par, 6)}
+        site[0] = t + 1
+        fw, bw, lf, lb = [("f0s", "b0s", "lfo0", "lbo0"), ("fin1", "bo0", "lfi1", "lbo1"), ("fin2", "bo1", "lfi2", "lbo0"), ("fin3", "bin3", "lfi3", "lbi3")][t]
+        par, nz_, pi_ = {1: ("parB", "nzB", "piB"), 2: ("parO", "nzO", "piO")}.get(t, ("par", "nzs", "pio"))
+        lam, rate = col(par, 4), {"f": col(par, 5), "b": col(par, 6)} if t in (1, 2) else {"f": col("neg", 0), "b": col("neg", 1)}
+        bent = A.add if t else A.subtract
+        def bend(x, o, bks, l_):
+            for h in (0, 1):
+                xh, bk = v(x, 512 * h, 512 * h + 512), bank(bks[h], 0, 512)
+                act(bk, v(x, 512 * h, 512 * h + 512, key=[xh[1], (l_, 0, 128)]) if l_[2] == "i" else xh, F.Square)
+                tt(v("mw", o + 512 * h, o + 512 * h + 512), xh, bk, bent, k=1)
+        olds = ((fw, K, lf), (bw, K + S, lb))
+        for x, o, l_ in olds:
+            if (t, l_[1]) in OPT["early"]:
+                bend(x, o, OPT["bb_"] if t else (2, 3), l_)
         for c in range(4):
-            cp(v("mw", 2 * K + 512 * c, 2 * K + 512 * c + 512), ind(v(bw, 0, S), v(lb, 32 * c, 32 * c + 32)), k=GA, eng=BOTH)
+            cp(v("ba", 512 * c, 512 * c + 512), ind(v(bw, 0, S), v(lb, 32 * c, 32 * c + 32)), k=GA, eng=BOTH)
         for c in range(4):
-            cp(v("mw", K + 512 * c, K + 512 * c + 512), ind(v(fw, 0, S), v(lf, 32 * c, 32 * c + 32)), k=GA, eng=BOTH)
+            cp(v("fi", 512 * c, 512 * c + 512), ind(v(fw, 0, S), v(lf, 32 * c, 32 * c + 32)), k=GA, eng=BOTH)
         umat("z", (4, 5))
         for c in range(4):
             lo, hi = 512 * c, 512 * c + 512
-            fi = v("mw", K + lo, K + hi)
-            tt(v("dd", lo, hi), ind(v("mw", 2 * K, 3 * K), v(pi_, 32 * c, 32 * c + 32)), fi, A.subtract, k=GA)
-            mul(bank(c % 2, 0, 512), v("dd", lo, hi), lam)
-            tt(v("mw", lo, hi), fi, bank(c % 2, 0, 512), A.add, k=1)
-            hits("mw", lo, lo, par, t, c == 3)
+            fi, bk = v("fi", lo, hi), bank(c, 0, 512)
+            tt(v("dd", lo, hi), ind(v("ba", 0, K), v(pi_, 32 * c, 32 * c + 32)), fi, A.subtract, k=GA)
+            if OPT["padd"][c]:
+                mms([(bk, mat("idf"), fi, True, False)], k=4)
+                mul(v("tb", lo, hi), v("dd", lo, hi), lam, BOTH)
+                mms([(bk, mat("idf"), v("tb", lo, hi), False, True)], k=4)
+                hits("bk%d" % c, 0, lo, par, t, c == 3)
+                act(v("sm", lo, hi), bk, F.Square)
+                tt(v("mw", lo, hi), bk, v("sm", lo, hi), bent, k=1)
+            else:
+                mul(bk, v("dd", lo, hi), lam, BOTH)
+                tt(v("tb", lo, hi), fi, bk, A.add, k=1)
+                hits("tb", lo, lo, par, t, c == 3)
+                act(bk, v("tb", lo, hi), F.Square)
+                tt(v("mw", lo, hi), v("tb", lo, hi), bk, bent, k=1)
             if c % 2:
                 counts(6, 64 * (c // 2), S * (c // 2))
-        ts(mat("wz"), bank(6, 0, 128), 8.5, A.is_ge)
-        we, wo = v("wz", 0, 128, 2), v("wz", 1, 128, 2)
-        mms([(bank(6, 128, 192), mat("two"), we, True, False), (bank(6, 128, 192), mat("two"), wo, False, True),
-             (bank(6, 200, 264), mat("me"), we, True, False), (bank(6, 200, 264), mat("mo"), wo, False, True)])
-        scan(v("csz", 64, 128), v("ones", 0, 64), bank(6, 128, 192), 0.0, A.mult, A.add)
-        tt(v("csz", 0, 64), v("csz", 64, 128), bank(6, 200, 264), A.subtract, k=1)
-        lin(v("cbz", 80, 144), v("csz", 0, 64), 1.0 / 32, 128.515625)
-        lin(v("ttz", 0, 64), v("cbz", 80, 144), 32.0, -129.0 * 32)
+        fl = {}
+        for p, l_ in (("f", lf), ("b", lb)):
+            fl[p] = mat("aa" + p) if l_[2] == "o" else mat("l%sl" % p)
+            if l_[2] == "i":
+                cp(fl[p], mat(l_))
+        mms([(bank(7, 256, 384), mat("evn"), fl["f"], True, False), (bank(7, 256, 384), mat("odd"), fl["b"], False, True)], k=4)
+        lin(mat("fcn"), bank(7, 256, 384), 1.0, col("kf", 6))
+        for x, o, l_ in olds:
+            if (t, l_[1]) not in OPT["early"]:
+                bend(x, o, OPT["lb_"][t], l_)
+        ts(v("wz", 2, 130), bank(6, 0, 128), 8.5, A.is_ge)
+        we, wo, pe_, po_ = v("wz", 2, 130, 2), v("wz", 3, 130, 2), v("wz", 0, 128, 2), v("wz", 1, 128, 2)
+        mms([(bank(6, 200, 264), mat("ne"), we, True, False), (bank(6, 200, 264), mat("no"), wo, False, False),
+             (bank(6, 200, 264), mat("me"), pe_, False, False), (bank(6, 200, 264), mat("mo"), po_, False, True),
+             (bank(6, 128, 192), mat("two"), we, True, False), (bank(6, 128, 192), mat("two"), wo, False, True)])
+        for e in OPT["zs"]:
+            scan(v("csz", 64 * e, 64 * e + 64), v("ones", 0, 64), bank(6, 128, 192) if e else bank(6, 200, 264), 0.0 if e else -15.5, A.mult, A.add)
+        ts(v("ttz", 0, 64), v("csz", 0, 64), 1.5 * 2 ** 28, A.add, 1.5 * 2 ** 28, A.subtract)
+        lin(v("cbz", 80, 144), v("csz", 0, 64), 1.0 / 32, 129.0)
         tt(v("lowz", 0, 64), v("csz", 0, 64), v("ttz", 0, 64), A.subtract)
-        invert("z", "b", (4, 5), 6, v("csz", 64, 128), 8)
+        invert("z", "b", (4, 5), 6, v("csz", 64, 128), ("thr", 8))
+        ts(mat("fbk"), mat("nq"), col("csz", 127), A.is_ge)
+        tt(mat("fbk"), mat("fbk"), mat("fcn"), A.mult)
         if last:
             for c in range(4):
                 x = v("dd", 512 * c, 512 * c + 512)
-                add(list(BOTH), lambda q, e, x=x: q.activation(x[0], x[0], F.Square) if e == "act" else q.tensor_tensor(x[0], x[0], x[0], A.mult),
-                    cost(512, 1.4), rs(x), rs(x))
-                act(x, x, F.Exp, scale=-1.0, extra=1.3 if c == 0 else 0.0)
-                mms([(bank(7, 0, Z), mat("idf"), v("dd", Z * j, Z * j + Z), j == 0, j == 7) for j in (2 * c, 2 * c + 1)], k=4)
+                if c in OPT["ysq"]:
+                    tt(x, x, x, A.mult)
+                else:
+                    act(x, x, F.Square)
+                if c % 2 == 0:
+                    act(x, x, F.Exp, scale=-1.0)
+                    continue
+                y, bk = v("dd", 512 * c - 512, 512 * c), bank(OPT["yb"][c // 2], 0, 512)
+                act(bk, x, F.Exp, scale=-1.0)
+                tt(y, y, bk, A.add, k=1)
+                for j in (2 * c - 2, 2 * c - 1):
+                    mms([(bank(7, 0, Z), mat("idf"), v("dd", Z * j, Z * j + Z), j == 0, j == 5)], k=4)
             cp(v("yes", 0, Z), bank(7, 0, Z), eng=BOTH)
             dma("sp", T.ye[:], T.yes[:], 2.2, r=[("yes", 0, Z)])
-        first, second = ("f", "b") if t == 1 else ("b", "f")
-        for p, sb in ((first, 6), (second, 2)):
-            mms([(bank(sb, 288, 352), mat("p%s0" % p), v("aaz", 0, 128, 2), True, False), (bank(sb, 288, 352), mat("p%s1" % p), v("aaz", 1, 128, 2), False, True)], k=4)
+        first, second = ("f", "b") if t < 2 else ("b", "f")
+        for p, sb in ((first, 6), (second, 5 if last else 7)):
+            for src in ("fbk", "aaz"):
+                mms([(bank(sb, 288, 352), mat("p%s%d" % (p, e)), v(src, e, 128, 2), src == "fbk" and not e, src == "aaz" and e == 1) for e in (0, 1)], k=4)
             cp(v("lo" + p, 0, 64), bank(sb, 288, 352))
-        for p, pb in ((first, (0, 1)), (second, (2, 3))):
+        for p, pb in ((first, OPT["pb"][0]), (second, OPT["pb"][1])):
             po = "%so%d" % (p, t % 2)
-            bias[0] = (OPT["bb"] if t == 2 else OPT["bs"]) if p == first else 0.0
             sh = p == "b" and not last
-            dst = (prv if p == "b" else nxt) if t == 2 else opp if p == first else None
+            dst = (nxt if p == "b" else prv) if t == 2 else opp if p == first else None
             sc = OPT["scl" if last else "sc"][0 if p == first else 1]
             for h, (lo, hi) in enumerate(zip(sc, sc[1:])):
-                hv = ind(v("mw", 0, 3 * K if p == "b" else 2 * K), v("lo" + p, lo // 16, hi // 16))
+                hv = ind(v("mw", 0, 2 * K if p == "b" else K + S), v("lo" + p, lo // 16, hi // 16))
                 x = v("sq" + p, lo, hi)
-                bk = bank(pb[h % 2], 0, hi - lo)
-                mms([(bk, mat("shb" if sh else "idb"), v(nz_, lo, hi), True, False)])
-                act(x, hv, F.Square, k=GA)
-                tt(x, hv, x, A.subtract, k=GA)
-                mul(x, x, rate[p], BOTH)
-                mms([(bk, mat("shf" if sh else "idf"), x, False, True)], k=4)
-                ts(v(po, lo, hi), bk, 0.0, A.max, 1.0, A.min)
+                bk = bank(pb[h % len(pb)], 0, hi - lo)
+                own = (t, p, h) in OPT["dadd"]
+                mms([(bk, mat("shb" if sh else "idb" if last else "idn"), v(nz_, lo, hi), True, own)])
+                mul(x, hv, rate[p], BOTH, k=GA)
+                if own:
+                    tt(x, x, bk, A.add, k=1)
+                else:
+                    mms([(bk, mat("shf" if sh else "idf"), x, False, True)], k=4)
+                ts(v(po, lo, hi), x if own else bk, 0.0 if last else -1.0, A.max, 1.0 if last else 0.0, A.min)
                 if last:
                     dma("sp", T["y" + p][:, lo:hi], T[po][:, lo:hi], 2.4, r=[(po, lo, hi)])
                 elif dst is not None and hi % 512 == 0:
-                    send(dst, v("%sin%d" % (p, t + 1), hi - 512, hi), v(po, hi - 512, hi), "%s%s%d" % (p, "ab"[hi // S], t + 1), OPT["tl"] * (1 + hi // S / 4))
+                    send(dst, v("%sin%d" % (p, t + 1), hi - 512, hi), v(po, hi - 512, hi), "%s%s%d" % (p, "ab"[hi // S], t + 1), tm["tl"] * (1 + hi // S / 3))
             if not last:
                 lst = "l%so%d" % (p, (t + 1) % 2)
-                ancestors(p, po, {"b": "parB", "f": "parF"}[p] if t != 1 else {"b": "par", "f": "parO"}[p], t + 1, lst,
-                          (4, 5) if p == first else (0, 1), 6 if p == first else 7, 0 if p == first else S)
+                ancestors(p, po, {"b": ("parB", "parO", "parF"), "f": ("parF", "par", "parB")}[p][t], t + 1, lst,
+                          OPT["ub"][p != first], 6 if p == first else 7, 0 if p == first else S, OPT["hc"][p != first])
                 if dst is not None:
-                    send(dst, mat("l%si%d" % (p, t + 1)), mat(lst), "%sl%d" % (p, t + 1), OPT["ll"])
+                    send(dst, mat("l%si%d" % (p, t + 1)), mat(lst), "%sl%d" % (p, t + 1), tm["ll"])
+                if t == 0 and p == second:
+                    for to, frm, w_ in (("piO", "pio", 128), ("nzO", "nzs", S)):
+                        send(opp, v(to, 0, w_), v(frm, 0, w_, key=[(frm, 0, w_), ("lfi1", 0, 128)]), to, 12.0)
     return ops
 
 
-def lay(ops, links, key, back, fixed):
-    HOP = OPT["hop"]
-    n = len(ops)
-    ins, outs = links[back], links[1 - back]
-    left = [len(x) for x in ins]
-    cand = [i for i in range(n) if not left[i]]
-    busy = {e: [] for e in ("pe", "dve", "act", "pool", "sp")}
-    start, end = [0.0] * n, [0.0] * n
+def lay(key, eng, loose, dur, rel, ins, outs, free):
+    m = len(dur)
+    left = [len(y) for y in ins]
+    cand = [(key[k], k) for k in range(m) if not left[k]]
+    busy = {e: [(0.0, free[e])] for e in QUEUES}
+    end = [0.0] * m
     while cand:
-        i = min(cand, key=lambda y: key[y])
-        cand.remove(i)
-        o, e = ops[i], fixed[i]
-        r = o["lat"] if back else 0.0
-        for j, kd in ins[i]:
-            a, b = (o, ops[j]) if back else (ops[j], o)
-            free = kd == "model" or (a["kind"] == "c" and b["kind"] == "c" and fixed[j] == e and (kd == "order" or e == "pe"))
-            x = end[j] if free else end[j] + a["lat"] + HOP
-            if x > r:
-                r = x
-        if e is not None:
-            B = busy[e]
-            k = len(B)
-            while k and B[k - 1][1] > r:
-                k -= 1
-            while k < len(B) and B[k][0] < r + o["dur"] - 1e-9:
-                r = max(r, B[k][1])
-                k += 1
-            B.insert(k, (r, r + o["dur"]))
-        start[i], end[i] = r, r + o["dur"]
-        for j, _k in outs[i]:
+        c = min(cand)
+        cand.remove(c)
+        k = c[1]
+        d, got = dur[k], None
+        for e in (("act", "dve") if k in loose else (eng[k],)):
+            r, u = rel[k][e], 0
+            for j, g1, g2 in ins[k]:
+                y = end[j] + (g1 if eng[j] == e else g2)
+                if y > r:
+                    r = y
+            if e:
+                B = busy[e]
+                u = len(B)
+                while u and B[u - 1][1] > r:
+                    u -= 1
+                while u < len(B) and B[u][0] < r + d - 1e-9:
+                    if B[u][1] > r:
+                        r = B[u][1]
+                    u += 1
+            if got is None or r < got[0] - 1e-9:
+                got = (r, e, u)
+        r, e, u = got
+        eng[k] = e
+        if e:
+            busy[e].insert(u, (r, r + d))
+        end[k] = r + d
+        for j, g1, g2 in outs[k]:
             left[j] -= 1
             if not left[j]:
-                cand.append(j)
-    return start, end, fixed
+                cand.append((key[j], j))
+    return end
 
 
-def greedy(ops):
-    HOP = OPT["hop"]
-    n = len(ops)
-    if "succ" not in ops[0]:
-        succ = [[] for _ in range(n)]
+def replay(seq, eng, dur, rel, ins, free):
+    fr = dict(free)
+    fr[None] = 0.0
+    end = [0.0] * len(dur)
+    for k in seq:
+        e = eng[k]
+        r = rel[k][e]
+        if e and fr[e] > r:
+            r = fr[e]
+        for j, g1, g2 in ins[k]:
+            y = end[j] + (g1 if eng[j] == e else g2)
+            if y > r:
+                r = y
+        end[k] = fr[e] = r + dur[k]
+    return end, fr
+
+
+def plan(T, topo, core):
+    alts = [build(T, topo, core, tm) for tm in SETS]
+    ops = alts[0]
+    n, sets = len(ops), range(len(SETS))
+    dur = [[o["dur"] for o in a] for a in alts]
+    lat = [[o["lat"] for o in a] for a in alts]
+    ins, outs = [[[] for _ in ops] for s in sets], [[[] for _ in ops] for s in sets]
+    for s in sets:
         for i, o in enumerate(ops):
-            for j in o["deps"]:
-                succ[j].append(i)
-        way = [0.0] * n
-        for i in range(n - 1, -1, -1):
-            way[i] = ops[i]["dur"] + ops[i]["lat"] + max([way[j] + HOP for j in succ[i]] + [0.0])
-        ops[0]["succ"], ops[0]["way"] = succ, way
-    succ = ops[0]["succ"]
-    prio = [ops[0]["way"][i] + ops[i]["bias"] + OPT["nudge"].get(ops[i]["site"], 0.0) for i in range(n)]
-    left = [len(o["deps"]) for o in ops]
-    cand = [i for i in range(n) if left[i] == 0]
-    free = {e: 0.0 for e in ("pe", "dve", "act", "pool", "sp")}
-    engs = [[OPT["force"][o["site"]]] if o["site"] in OPT["force"] else o["eng"] for o in ops]
-    order = []
-    memo = {}
-
-    def ready(i, e):
-        if (i, e) not in memo:
-            r = 0.0
-            for j, kd in ops[i]["deps"].items():
-                o = ops[j]
-                if kd == "model" or (o["kind"] == "c" and o["on"] == e and (kd == "order" or e == "pe")):
-                    r = max(r, o["end"])
-                else:
-                    r = max(r, o["done"] + HOP)
-            memo[(i, e)] = r
-        return memo[(i, e)]
-
-    def place(i, e, st):
-        o = ops[i]
-        o["on"] = e; o["start"] = st; o["end"] = st + o["dur"]; o["done"] = o["end"] + o["lat"]
-        if e is not None:
-            free[e] = o["end"]
-        order.append(i)
-        cand.remove(i)
-        for j in succ[i]:
-            left[j] -= 1
-            if left[j] == 0:
-                cand.append(j)
-
-    while cand:
-        arr = [i for i in cand if ops[i]["kind"] == "arr"]
-        if arr:
-            place(arr[0], None, ready(arr[0], None))
-            continue
-        opts = [(max(free[e], ready(i, e)), i, e) for i in cand for e in engs[i]]
-        t0, _, e0 = min(opts)
-        def rank_(y):
-            return (prio[y[1]] - (OPT["pen"] if len(engs[y[1]]) > 1 and y[2] == "dve" else 0.0), -y[1])
-        now = [y for y in opts if y[2] == e0 and y[0] <= t0 + 1e-9]
-        b = max(now, key=rank_)
-        soon = [y for y in opts if y[2] == e0 and t0 + 1e-9 < y[0] < t0 + OPT["look"] * ops[b[1]]["dur"] and rank_(y)[0] > rank_(b)[0] + OPT["margin"]]
-        if soon:
-            u = max(soon, key=rank_)
-            fit = [y for y in now if ops[y[1]]["dur"] <= u[0] - t0 + 0.03]
-            b = max(fit, key=rank_) if fit else u
-        place(b[1], b[2], b[0])
-    return order
-
-
-def replay(ops, order, on, hop):
-    free = {}
-    end = [0.0] * len(ops)
-    for i in order:
-        o, e = ops[i], on[i]
-        r = free.get(e, 0.0) if e else 0.0
-        for j, kd in o["deps"].items():
-            d = ops[j]
-            r = max(r, end[j] if kd == "model" or (d["kind"] == "c" and on[j] == e and (kd == "order" or e == "pe")) else end[j] + d["lat"] + hop)
-        end[i] = r + o["dur"]
-        if e:
-            free[e] = end[i]
-    return max(end[i] + o["lat"] for i, o in enumerate(ops))
-
-
-def tune(T, topo, core):
-    base = dict(OPT)
-    ops = build(T, topo, core)
-    alts = []
-    for s in SETS:
-        OPT.update(s)
-        alts.append(build(T, topo, core))
-        OPT.update(base)
-    sites = sorted({o["site"] for o in ops if o["kind"] != "arr"})
-    x = [12345]
-
-    def pick(seq):
-        x[0] = (x[0] * 1103515245 + 12345) % 2147483648
-        return seq[(x[0] >> 8) % len(seq)]
-
-    fsite = sorted({o["site"] for o in ops if len(o["eng"]) > 1})
-
-    def total(order, on):
-        return sum(replay(a, order, on, s["hop"]) for a, s in zip(alts, SETS))
-
-    def score(nudge, force):
-        OPT["force"] = force
-        OPT["nudge"] = nudge
-        order = greedy(ops)
-        return total(order, [o["on"] for o in ops])
-    cur = {}
-    frc = {}
-    best = score(cur, frc)
-    for _ in range(OPT["first"]):
-        c = dict(cur)
-        for _k in range(pick((1, 2, 3, 5))):
-            a, d = pick(range(len(sites))), pick((-3, -1.5, -0.7, -0.3, 0.3, 0.7, 1.5, 3))
-            for y in sites[a:a + pick((1, 1, 2, 4, 8))]:
-                c[y] = c.get(y, 0.0) + d
-        f_ = dict(frc)
-        if pick((0, 0, 1)):
-            c = dict(cur)
-            for _k in range(pick((1, 1, 2))):
-                f_[pick(fsite)] = pick(("act", "dve"))
-        s = score(c, f_)
-        if s <= best:
-            best, cur, frc = s, c, f_
-    OPT["nudge"] = cur
-    OPT["force"] = frc
-    n = len(ops)
-    ins = [list(o["deps"].items()) for o in ops]
-    outs = [[] for _ in ops]
-    for i in range(n):
-        for j, kd in ins[i]:
-            outs[j].append((i, kd))
-    links = (ins, outs)
-    x[0] = OPT["seed"]
+            for j, kd in o["deps"].items():
+                g2 = 0.0 if kd == "model" else lat[s][j] + SETS[s]["hop"]
+                g1 = 0.0 if ops[j]["kind"] == o["kind"] == "c" and (kd == "order" or o["eng"][0] == "pe") else g2
+                ins[s][i].append((j, g1, g2))
+                outs[s][j].append((i, g1, g2))
+    x = [OPT["seed"]]
 
     def rnd():
         x[0] = (x[0] * 1103515245 + 12345) % 2147483648
         return x[0] / 2147483648.0
-    order = greedy(ops)
-    on = [o["on"] for o in ops]
-    best = (total(order, on), order, on, [o["start"] for o in ops], [o["end"] for o in ops])
-    flex = [i for i in range(n) if len(ops[i]["eng"]) > 1]
+
+    zero = dict.fromkeys(QUEUES, 0.0)
+    none = [dict.fromkeys(o["eng"], 0.0) for o in ops]
+    tail = [[dict.fromkeys(o["eng"], lat[s][i]) for i, o in enumerate(ops)] for s in sets]
+    on = [o["eng"][0] for o in ops]
+    key = [0.0] * n
+    for i in range(n - 1, -1, -1):
+        key[i] = min([key[j] - g2 for j, g1, g2 in outs[0][i]] + [-lat[0][i]]) - dur[0][i]
+    for _ in range(3):
+        end = lay(key, on, (), dur[0], none, ins[0], outs[0], zero)
+        key = [-y for y in lay([-y for y in end], on, (), dur[0], tail[0], outs[0], ins[0], zero)]
+    end = lay(key, on, (), dur[0], none, ins[0], outs[0], zero)
+    order = sorted(range(n), key=lambda i: (end[i] - dur[0][i], i))
+    other = {"act": "dve", "dve": "act"}
+    width, inner = OPT["width"], OPT["inner"]
     for it in range(OPT["tries"]):
-        on, key = list(best[2]), best[3]
-        t0, amp, u = rnd() * max(key), OPT["amp"] * rnd(), rnd()
-        if u < 0.4:
-            i = flex[int(rnd() * len(flex))]
-            on[i] = "act" if on[i] == "dve" else "dve"
-        if u > 0.3:
-            key = [y + (amp * rnd() if t0 < y < t0 + OPT["span"] else 0.0) for y in key]
-        if rnd() < OPT["back"]:
-            _s, back, _o = lay(ops, links, [-y for y in key], 1, on)
-            key = [-y for y in back]
-        st, en, on = lay(ops, links, key, 0, on)
-        order = sorted(range(n), key=lambda i: (st[i], i))
-        sc = total(order, on)
-        if sc <= best[0]:
-            best = (sc, order, on, st, en)
-    OPT["plan"] = best
-    OPT["tries"] = 0
-    OPT["best"] = best[0] / len(SETS)
+        head = [replay(order, on, dur[s], none, ins[s], zero)[0] for s in sets]
+        order.sort(key=lambda i: (head[0][i] - dur[0][i], i))
+        a = int(rnd() * (n + width / 2) - width / 2)
+        a, b = max(a, 0), min(n, a + width)
+        W = order[a:b]
+        m = len(W)
+        loc = {i: k for k, i in enumerate(W)}
+        late = set(order[b:])
+        rel, out, pin, pout, dw, free, after, base = [], [], [], [], [], [], [], []
+        for s in sets:
+            q, nx = replay(order[:b - 1:-1] if b < n else [], on, dur[s], tail[s], [[y for y in z if y[0] in late] for z in outs[s]], zero)
+            fr = dict(zero)
+            for i in order[:a]:
+                fr[on[i]] = head[s][i]
+            base.append(max([0.0] + [head[s][i] + (g1 if on[i] == on[j] else g2) + q[j] for i in order[:a] for j, g1, g2 in outs[s][i] if j in late]))
+            rel.append([{e: max([0.0] + [head[s][j] + (g1 if on[j] == e else g2) for j, g1, g2 in ins[s][i] if j not in loc]) for e in ops[i]["eng"]} for i in W])
+            out.append([{e: max([lat[s][i]] + [q[j] + (g1 if on[j] == e else g2) for j, g1, g2 in outs[s][i] if j in late]) for e in ops[i]["eng"]} for i in W])
+            pin.append([[(loc[j], g1, g2) for j, g1, g2 in ins[s][i] if j in loc] for i in W])
+            pout.append([[(loc[j], g1, g2) for j, g1, g2 in outs[s][i] if j in loc] for i in W])
+            dw.append([dur[s][i] for i in W])
+            free.append(fr); after.append(nx)
+        flex = [k for k, i in enumerate(W) if len(ops[i]["eng"]) > 1]
+
+        def score(seq, eng):
+            tot = 0.0
+            for s in reversed(sets):
+                end, fr = replay(seq, eng, dw[s], rel[s], pin[s], free[s])
+                top = max([base[s]] + [y + o[e] for y, o, e in zip(end, out[s], eng)] + [fr[e] + after[s][e] for e in QUEUES])
+                tot += SETS[s]["wt"] * (top + 0.01 * sum(end) / m)
+            return (tot, seq, eng, [y - d for y, d in zip(end, dw[0])])
+
+        cur = score(list(range(m)), [on[i] for i in W])
+        best = (cur[0] + OPT["slack"] * max(0.0, 1 - 1.4 * it / OPT["tries"]) * rnd(),) + cur[1:]
+        for step in range(inner):
+            eng, key, u = list(cur[2]), list(cur[3]), rnd()
+            if u < 0.3 and flex:
+                k = flex[int(rnd() * len(flex))]
+                eng[k] = other[eng[k]]
+                j = flex[int(rnd() * len(flex))]
+                if u < 0.1 and eng[j] == eng[k] and j != k:
+                    eng[j] = other[eng[j]]
+            if u > 0.75:
+                i0, d = W[int(rnd() * m)], 4 * (rnd() - 0.5)
+                i1 = i0 + 2 + int(rnd() * rnd() * 60)
+                key = [y + (d if i0 <= W[k] < i1 else 0.0) for k, y in enumerate(key)]
+            elif u > 0.6:
+                t0, am = key[int(rnd() * m)], rnd()
+                key = [y + (am * rnd() if t0 < y < t0 + 2.0 else 0.0) for y in key]
+            elif u > 0.2:
+                for _ in range(1 + int(rnd() * 2)):
+                    key[int(rnd() * m)] += 3 * (rnd() - 0.5)
+            if rnd() < 0.6:
+                key = [-y for y in lay([-y - d for y, d in zip(key, dw[0])], eng, (), dw[0], out[0], pout[0], pin[0], after[0])]
+            loose = ()
+            if rnd() < 0.3:
+                t0, sp = cur[3][int(rnd() * m)], 4 * rnd()
+                loose = {k for k in flex if t0 <= cur[3][k] < t0 + sp}
+            end = lay(key, eng, loose, dw[0], rel[0], pin[0], pout[0], free[0])
+            c = score(sorted(range(m), key=lambda k: (end[k] - dw[0][k], W[k])), eng)
+            if c[0] <= cur[0] + OPT["temp"] * (1 - it / OPT["tries"]) * (1 - step / inner) * rnd():
+                cur = c
+                if c[0] < best[0] and 3 * step > inner:
+                    best = c
+        order[a:b] = [W[k] for k in best[1]]
+        for k, i in enumerate(W):
+            on[i] = best[2][k]
+    ends = [replay(order, on, dur[s], none, ins[s], zero)[0] for s in sets]
+    return order, on, [[y + z for y, z in zip(ends[s], lat[s])] for s in sets]
 
 
-def schedule(ops):
-    _, order, on, st, en = OPT["plan"]
-    for i, o in enumerate(ops):
-        o["on"] = on[i]; o["start"] = st[i]; o["end"] = en[i]; o["done"] = en[i] + o["lat"]
-    return order
+PLAN = []
 
 
 def rank_program(g, core, T, topo):
     if T.rank_of(core) is None:
         return
-    if OPT["tries"]:
-        tune(T, topo, core)
-    ops = build(T, topo, core)
-    order = schedule(ops)
+    if not PLAN:
+        PLAN.extend(plan(T, topo, core))
+    order, on, done = PLAN
+    ops = build(T, topo, core, SETS[0])
     Q = {"pe": g.tensor, "dve": g.vector, "act": g.scalar, "pool": g, "sp": g.sync}
 
     def waits(i):
         o = ops[i]
-        out = []
-        for j, kd in o["deps"].items():
-            d = ops[j]
-            if kd == "model":
-                continue
-            if d["kind"] == "c" and o["kind"] == "c" and d["on"] == o["on"] and (kd == "order" or o["on"] == "pe"):
-                continue
-            out.append(j)
-        return out
+        return [j for j, kd in o["deps"].items()
+                if kd != "model" and not (ops[j]["kind"] == o["kind"] == "c" and on[j] == on[i] and (kd == "order" or on[i] == "pe"))]
 
     pos = {}
     seen = {e: 0 for e in Q}
     for i in order:
         if ops[i]["kind"] == "c":
-            seen[ops[i]["on"]] += 1
-            pos[i] = seen[ops[i]["on"]]
+            seen[on[i]] += 1
+            pos[i] = seen[on[i]]
     know = {e: {} for e in Q}
     after = {}
     need = {}
@@ -660,11 +683,11 @@ def rank_program(g, core, T, topo):
         if o["kind"] == "arr":
             after[i] = {o["sem"]: 1}
             continue
-        kn = know[o["on"]]
+        kn = know[on[i]]
         lst = []
-        for j in sorted(waits(i), key=lambda j: -ops[j]["done"]):
+        for j in sorted(waits(i), key=lambda j: -done[0][j]):
             d = ops[j]
-            key, val = (d["on"], pos[j]) if d["kind"] == "c" else (d["sem"], 1)
+            key, val = (on[j], pos[j]) if d["kind"] == "c" else (d["sem"], 1)
             if kn.get(key, 0) >= val:
                 continue
             lst.append(j)
@@ -675,7 +698,7 @@ def rank_program(g, core, T, topo):
         need[i] = lst
         a = dict(kn)
         if o["kind"] == "c":
-            a[o["on"]] = pos[i]
+            a[on[i]] = pos[i]
         else:
             a[o["sem"]] = 1
         after[i] = a
@@ -685,11 +708,11 @@ def rank_program(g, core, T, topo):
         o = ops[i]
         if o["kind"] == "arr":
             continue
-        e = o["on"]
+        e = on[i]
         for j in need[i]:
             d = ops[j]
             if d["kind"] == "c":
-                Q[e].wait_ge(T.sem[d["on"]], val[j])
+                Q[e].wait_ge(T.sem[on[j]], val[j])
             else:
                 Q[e].wait_ge(T.sem[d["sem"]], d["cnt"])
         ins = o["fn"](Q[e], e)
@@ -698,7 +721,7 @@ def rank_program(g, core, T, topo):
                 count[e] += 1
                 val[i] = count[e]
                 ins.then_inc(T.sem[e], 1)
-        elif e != "pool":
+        elif o["kind"] == "dma":
             ins.then_inc(T.sem[o["sem"]], 16)
     for o in ops:
         if o["kind"] != "c":

from concourse.bass import DstId, RemoteDMATransfer
from concourse.mybir import AluOpType, ActivationFunctionType

A = AluOpType
F = ActivationFunctionType
S, K, RO, Z = 1024, 2048, 4, 256
GAP = 32.5 / 128
f32, b16, u16, i32 = "float32", "bfloat16", "uint16", "int32"

SCRATCH = {}


def _sb(name, n, d=f32):
    SCRATCH[name] = ("sbuf", [128, n], d)


for _n in ("f0s", "b0s", "nzs"):
    _sb(_n, S, b16)
for _n in ("f%s1", "f%s2", "f%s3", "b%s3"):
    _sb(_n % "in", S); _sb("l" + _n % "i", 128, u16)
for _t in (0, 1):
    _sb("fo%d" % _t, S); _sb("bo%d" % _t, S)
    _sb("lfo%d" % _t, 128, u16); _sb("lbo%d" % _t, 128, u16)
_sb("neg", 4); _sb("par", 8); _sb("parF", 8); _sb("parB", 8); _sb("parO", 8)
_sb("nzB", S, b16); _sb("nzO", S, b16); _sb("piB", 128, u16); _sb("piO", 128, u16); _sb("pis", 128, i32); _sb("pio", 128, u16)
_sb("mw", 2 * K); _sb("fi", K); _sb("ba", K); _sb("tb", K); _sb("sm", K); _sb("dd", K); _sb("ab", K); _sb("hh", K, b16)
_sb("lfl", 128); _sb("lbl", 128); _sb("yes", Z)
for _p in "fbz":
    _sb("w" + _p, 136, b16); _sb("cs" + _p, 144); _sb("cb" + _p, 160, b16); _sb("tt" + _p, 64)
    _sb("low" + _p, 128, b16); _sb("na" + _p, 8); _sb("no" + _p, 8, u16); _sb("zz" + _p, 256, b16); _sb("jo" + _p, 8, u16)
    _sb("jr" + _p, 136); _sb("aa" + _p, 128); _sb("js" + _p, 128)
for _p in "fb":
    _sb("sq" + _p, S); _sb("vv" + _p, 1032); _sb("lo" + _p, 64, u16); _sb("rr" + _p, 4); _sb("rho" + _p, 64)
_sb("junk", 1536, b16); _sb("fbk", 128); _sb("nq", 128); _sb("fcn", 128); _sb("seg", 128)
_sb("sel", 144, b16); _sb("rep", 2048, b16); _sb("rep8", 1024, b16); _sb("rc8", 8); _sb("hm", 4); _sb("itab", 1032)
_sb("cr", S, b16); _sb("cla", 128, b16); _sb("clz", 128, b16)
_sb("ki", 4, i32); _sb("kf", 12); _sb("mrow", 144); _sb("dm", 128, b16); _sb("tmp", 128, b16); _sb("tm2", 128, b16); _sb("same", 128, b16)
_sb("amr", 128); _sb("thr", 16); _sb("cq", 128); _sb("ones", 72); _sb("c384", 136, b16); _sb("e0", 128); _sb("e1", 128)
PACK = {}
for _b, _d, _names in (("cm", b16, ("half", "suf", "two", "me", "mo", "ne", "no", "idb", "idn", "shb")),
                       ("cf", f32, ("pf0", "pf1", "pb0", "pb1", "idf", "shf", "evn", "odd"))):
    _sb(_b, 128 * len(_names), _d)
    PACK.update({_n: (_b, 128 * _k) for _k, _n in enumerate(_names)})
for _k in range(8):
    SCRATCH["bk%d" % _k] = ("psum", [128, 512], f32)

NDMA = 40
ARR = ["par", "nzB", "piB", "nzO", "piO"] + [n % k for n in ("f%s1", "f%s2", "f%s3", "b%s3") for k in "abl"]
SEMAPHORES = ["pe", "dve", "act", "pool"] + ["d%d" % k for k in range(NDMA)] + ARR

OPT = {"padd": (1, 0, 0, 0), "yb": (0, 1), "early": ((0, "b"), (1, "b"), (2, "b"), (3, "b")), "ysq": (), "zs": (0, 1), "lb_": ((7, 2), (7, 2), (7, 2), (7, 2)), "dadd": [(t, "f", h) for t in range(4) for h in range(4)] + [(3, "b", 0), (3, "b", 1)],
       "pb": ((0, 1, 2, 3), (4, 5)), "ub": ((0, 1), (2, 3)), "bb_": (4, 5), "hc": ((0, 256, 512, 768, 1024), (0, 512, 1024)),
       "sc": ((0, 256, 512, 768, 1024), (0, 512, 1024)), "scl": ((0, 512, 1024), (0, 512, 768, 1024)),
       "tries": 250, "inner": 200, "width": 150, "temp": 0.3, "slack": 0.0, "seed": 1}
SETS = [{"cy": 0.00083, "hop": 0.2, "fix": 0.02, "pec": 0.00042, "ll": 2.0, "tl": 4.0, "ga": 1.56, "wt": 1.0},
        {"cy": 0.00083, "hop": 0.2, "fix": 0.02, "pec": 0.00084, "ll": 2.0, "tl": 4.0, "ga": 1.3, "wt": 0.8},
        {"cy": 0.0011, "hop": 0.24, "fix": 0.03, "pec": 0.0006, "ll": 4.0, "tl": 8.0, "ga": 1.9, "wt": 0.4}]
QUEUES = ("pe", "dve", "act", "pool", "sp")


def build(T, topo, core, tm):
    CY, PEC, GA = tm["cy"], tm["pec"], tm["ga"]
    rank = T.rank_of(core)
    n = len(T.cores)
    nxt, prv = T.cores[(rank + 1) % n], T.cores[(rank - 1) % n]
    opp = T.cores[(rank + 2) % n]
    ops = []
    hist = {}
    lastbank = {}
    site = [0]
    BOTH = ("act", "dve")

    def add(eng, fn, dur, r=(), w=(), kind="c", lat=0.0, sem=None, cnt=0, after=()):
        i = len(ops)
        deps = {}
        for j in after:
            deps[j] = "model"
        for isw, lst in ((False, r), (True, w)):
            for (nm, lo, hi) in lst:
                h = hist.setdefault(nm, [])
                for (j, l2, h2, w2) in h:
                    if l2 < hi and lo < h2 and (isw or w2) and j != i:
                        deps[j] = "raw"
                if nm.startswith("bk"):
                    j = lastbank.get(nm)
                    if j is not None and j != i and j not in deps:
                        deps[j] = "order"
                    lastbank[nm] = i
                if isw:
                    h[:] = [y for y in h if not (lo <= y[1] and y[2] <= hi)]
                h.append((i, lo, hi, isw))
        ops.append({"eng": eng, "fn": fn, "dur": dur, "deps": deps, "kind": kind, "lat": lat, "sem": sem, "cnt": cnt,
                    "tag": (list(w) + list(r))[0], "site": site[0]})
        return i

    def v(nm, lo, hi, step=1, key=None):
        buf, o = PACK.get(nm, (nm, 0))
        ap_ = T[buf][:, o + lo:o + hi] if step == 1 else T[buf][:, o + lo:o + hi:step]
        return (ap_, (nm, lo, hi) if key is None else key, len(range(lo, hi, step)))

    def ind(win, off):
        return (win[0].indirect(off[0]), win[1], 16 * off[2], off[1])

    def rs(*xs):
        out = []
        for x in xs:
            if isinstance(x, tuple):
                out += x[1] if isinstance(x[1], list) else [x[1]]
                if len(x) > 3:
                    out.append(x[3])
        return out

    def ap(x):
        return x[0] if isinstance(x, tuple) else x

    def cost(n_, k=1.0):
        return tm["fix"] + max(64, n_ * k) * CY + (0.035 if k == GA else 0.0)

    def ts(out, in0, s1, op0, s2=None, op1=None, k=1.0):
        def fn(q, e):
            if op1 is None:
                return q.tensor_scalar(out[0], in0[0], ap(s1), None, op0)
            return q.tensor_scalar(out[0], in0[0], ap(s1), ap(s2), op0, op1)
        return add(["dve"], fn, cost(in0[2], k), rs(in0, s1, s2), rs(out))

    def tt(out, in0, in1, op, k=2.0):
        return add(["dve"], lambda q, e: q.tensor_tensor(out[0], in0[0], in1[0], op), cost(in0[2], k), rs(in0, in1), rs(out))

    def cp(out, in_, k=1.0, eng=("dve",)):
        def fn(q, e):
            if e == "dve":
                return q.tensor_copy(out[0], in_[0])
            return q.activation(out[0], in_[0], F.Copy)
        return add(list(eng), fn, cost(in_[2], k), rs(in_), rs(out))

    def mul(out, in_, c, eng=("act",), k=1.0):
        def fn(q, e):
            if e == "dve":
                return q.tensor_scalar(out[0], in_[0], ap(c), None, A.mult)
            return q.activation(out[0], in_[0], F.Identity, scale=ap(c))
        return add(list(eng), fn, cost(in_[2], k), rs(in_, c), rs(out))

    def lin(out, in_, scale, bias_):
        def fn(q, e):
            if e == "dve":
                return q.tensor_scalar(out[0], in_[0], ap(scale), ap(bias_), A.mult, A.add)
            return q.activation(out[0], in_[0], F.Identity, bias=ap(bias_), scale=ap(scale))
        return add(list(BOTH), fn, cost(in_[2]), rs(in_, scale, bias_), rs(out))

    def act(out, in_, func, bias=0.0, scale=1.0, acc=None, k=1.0, extra=0.0):
        def fn(q, e):
            if acc is None:
                return q.activation(out[0], in_[0], func, bias=ap(bias), scale=ap(scale))
            return q.activation(out[0], in_[0], func, bias=ap(bias), scale=ap(scale), accum_out=acc[0])
        return add(["act"], fn, cost(in_[2], k) + extra, rs(in_, bias, scale), rs(out, acc))

    def scan(out, d0, d1, init, op0, op1):
        return add(["dve"], lambda q, e: q.tensor_tensor_scan(out[0], d0[0], d1[0], ap(init), op0, op1), cost(out[2]), rs(d0, d1, init), rs(out))

    def ms(out, c, k=1.0):
        return add(["dve"], lambda q, e: q.memset(out[0], c), cost(out[2], k), [], rs(out))

    def mms(items, k=1):
        def fn(q, e):
            return [q.matmul(o[0], l[0], r[0], st, sp) for (o, l, r, st, sp) in items][-1]
        return add(["pe"], fn, sum(0.004 + max(64, x[2][2]) * k * PEC for x in items), [y for x in items for y in rs(x[1], x[2])], [y for x in items for y in rs(x[0])])

    def iota(out, pat, base, cm, integer=False):
        def fn(q, e):
            if integer:
                return q.iota(out[0], pat, base, cm)
            return q.iota(out[0], pat, base, cm, allow_small_or_imprecise_dtypes=True)
        return add(["pool"], fn, 0.13 + 2 * CY * out[2], [], rs(out) + [("poolq", 0, 1)])

    nd = [0]

    def dsem():
        nd[0] += 1
        return "d%d" % (nd[0] - 1)

    def dma(q_, out, in_, lat, r=(), w=()):
        return add([q_], lambda q, e: q.dma_start(out, in_), 0.06, r, w, kind="dma", lat=lat, sem=dsem(), cnt=16)

    narrow = min((topo.engines(core, d) for d in (nxt, prv)), key=len)
    emask = {}
    for d in (nxt, prv, opp):
        es = topo.engines(core, d)
        rest = [e for e in es if e not in narrow]
        emask[d] = rest if rest else es

    def send(dst, out, in_, rsem, lat):
        rid, pid = topo.addr(dst, core)
        es = emask[dst]
        m = sum(1 << e for e in es)
        ls = dsem()
        i = add(["pool"], lambda q, e: q.remote_dma(out[0], in_[0], T.sem[rsem], T.sem[ls], pid, rid, m), 0.5, rs(in_), [],
                kind="far", lat=lat, sem=ls, cnt=len(es))
        add([None], None, 0.0, [], rs(out), kind="arr", lat=lat, sem=rsem, cnt=len(narrow), after=[i])

    def bank(k_, lo, hi, step=1):
        return v("bk%d" % k_, lo, hi, step)

    def col(nm, c):
        return v(nm, c, c + 1)

    def mat(nm):
        return v(nm, 0, 128)

    def rows(nm, p0, p1, key, width):
        return (T[nm][p0:p1, :], (nm, key, key + 1), width)

    dma("sp", T.b0s[:], T.b0[:], 2.6, w=[("b0s", 0, S)])
    dma("act", T.par[:, 0:4], T.obs[:], 2.0, w=[("par", 0, 4)])
    dma("act", T.par[:, 7:8], T.eps[:], 2.0, w=[("par", 7, 8)])
    dma("sp", T.f0s[:], T.f0[:], 3.0, w=[("f0s", 0, S)])
    dma("sp", T.pis[:], T.pi[:], 3.0, w=[("pis", 0, 128)])
    dma("sp", T.par[:, 4:5], T.lam[:], 3.0, w=[("par", 4, 5)])
    dma("sp", T.par[:, 5:6], T.rf[:], 3.0, w=[("par", 5, 6)])
    dma("sp", T.par[:, 6:7], T.rb[:], 3.0, w=[("par", 6, 7)])
    dma("sp", T.nzs[:], T.nz[:], 3.0, w=[("nzs", 0, S)])

    iota(v("ki", 0, 1), [[0, 1]], 0, 1, integer=True)
    iota(v("mrow", 0, 144), [[1, 144]], 0, 0)
    ts(col("ki", 1), col("ki", 0), 15, A.bitwise_and)
    cp(v("kf", 0, 2), v("ki", 0, 2))
    kk, ak = col("kf", 0), col("kf", 1)
    tt(col("kf", 2), kk, ak, A.subtract)
    ts(mat("dm"), mat("mrow"), col("kf", 2), A.subtract)
    dm = mat("dm")
    ts(mat("tmp"), dm, -0.5, A.is_gt, k=0.5)
    ts(mat("tm2"), dm, 15.5, A.is_lt, k=0.5)
    tt(mat("same"), mat("tmp"), mat("tm2"), A.mult, k=1)
    same = mat("same")
    ts(v("sel", 0, 144), v("mrow", 0, 144), col("kf", 2), A.subtract, 15.0, A.is_equal)
    mul(mat("half"), same, 0.5, BOTH)
    ts(mat("tmp"), dm, ak, A.is_lt, 0.5, A.mult, k=0.5)
    tt(mat("suf"), mat("tmp"), same, A.mult, k=1)
    ms(v("c384", 0, 64), -384.0); ms(v("c384", 64, 65), 0.0); ms(v("c384", 65, 66), GAP / 8); ms(v("c384", 72, 136), -GAP)
    ms(v("ones", 0, 64), 1.0); ms(v("ones", 64, 65), 1.0 / 128); ms(v("ones", 65, 66), -129.0)
    for p in "fb":
        ms(v("w" + p, 64, 66), 0.0); ms(v("vv" + p, 0, 1), 0.0)
    for p in "fbz":
        ms(v("jr" + p, 0, 1), 0.0)
    act(v("cbb", 144, 160), v("ones", 0, 16), F.Exp, scale=7.0, extra=1.3)
    for p in "fz":
        cp(v("cb" + p, 144, 160), v("cbb", 144, 160), eng=BOTH)
    ts(col("hm", 0), ak, 7.5, A.is_lt); ts(col("hm", 1), ak, 7.5, A.is_gt)
    ts(v("hm", 2, 4), v("hm", 0, 2), 12.0 + (0.5 - 2.0 ** -14) / 16, A.mult)
    ts(col("kf", 7), col("hm", 1), -8.0, A.mult, ak, A.add)
    ts(v("rc8", 0, 8), v("mrow", 0, 8), col("kf", 7), A.is_equal, -65536.0, A.mult)
    for a in range(8):
        mul(v("rep8", 128 * a, 128 * a + 128), same, col("rc8", a), BOTH)
    ms(v("wz", 0, 2), 0.0)
    ts(col("neg", 2), col("par", 0), -1.0, A.mult)
    ts(v("neg", 0, 2), v("par", 5, 7), -1.0, A.mult)
    iota(mat("amr"), [[0, 8], [2, 16]], 1, 0)
    iota(rows("cr", 0, 64, 0, S), [[0, S]], 2048, 0)
    iota(v("itab", 0, 1025), [[1, 1025]], 0, 0)
    iota(rows("cr", 64, 96, 1, S), [[16, 64], [0, 16]], 0, 0)
    iota(rows("cr", 96, 128, 2, S), [[0, 64], [2, 16]], 1, 0)
    mul(rows("cla", 0, 32, 0, 128), (T.amr[0:32, :], ("amr", 0, 128), 128), 1.0 / 32, BOTH)
    mul(rows("clz", 0, 32, 0, 128), (T.amr[0:32, :], ("amr", 0, 128), 128), 1.0, BOTH)
    for (nm, p0, c, key) in (("cla", 32, 12.0, 1), ("clz", 32, -15.5, 1), ("clz", 64, 1.0 / 32, 2), ("clz", 96, 1.0 / 64, 3)):
        ms(rows(nm, p0, p0 + 32, key, 64), c)
    ts(v("thr", 0, 8), v("mrow", 0, 128, 16), ak, A.add, 1.0, A.add)
    lin(v("thr", 8, 16), v("thr", 0, 8), 32.0, -0.5)
    lin(mat("cq"), mat("mrow"), 1.0, 129.5)
    ts(mat("idf"), dm, ak, A.is_equal)
    mul(mat("idb"), mat("idf"), 1.0, BOTH)
    ts(col("kf", 4), ak, 2.0, A.mult)
    ts(mat("e0"), mat("amr"), col("kf", 4), A.subtract, 1.0, A.is_equal)
    mul(mat("seg"), mat("e0"), 4096.0, BOTH)
    cp(mat("pio"), mat("pis"))
    ways = {}
    for dst, to in ((prv, "parF"), (nxt, "parB"), (opp, "parO")):
        ways.setdefault(sum(1 << e for e in emask[dst]), []).append((topo.addr(dst, core), to))
    ls = dsem()
    i = add(["pool"], lambda q, e: q.remote_dma_fused([
        RemoteDMATransfer(dst_ids=[DstId(rid=a[0], pnc=a[1]) for a, to in ds], dma_engine_mask=m, remote_sem=T.sem["par"], srcs=[T.par[:]], dsts=[T[to][:] for a, to in ds])
        for m, ds in ways.items()], local_sem=T.sem[ls]), 1.0, [("par", 0, 8), ("poolq", 0, 1)], [], kind="far", lat=6.0, sem=ls, cnt=len(narrow) * len(ways))
    add([None], None, 0.0, [], [(to, 0, 8) for to in ("parF", "parB", "parO")], kind="arr", lat=6.0, sem="par", cnt=3 * len(narrow), after=[i])
    for to, frm, w_ in (("nzB", "nzs", S), ("piB", "pio", 128)):
        send(nxt, v(to, 0, w_), v(frm, 0, w_, key=[(frm, 0, w_), ("poolq", 0, 1)]), to, 12.0)
    for h in (0, 1):
        mul(v("rep", S * h, S * h + S), v("rep8", 0, S), col("hm", h), ("dve",), k=0.5)
    mul(mat("two"), same, 2.0, BOTH)
    ts(mat("e0"), dm, -2.0, A.mult, ak, A.add)
    lin(mat("e1"), mat("e0"), 1.0, 16.0)
    for nm, e_, t_ in (("me", "e0", "tmp"), ("mo", "e1", "tm2")):
        ts(mat(t_), mat(e_), 0.0, A.max, 2.0, A.min)
        tt(mat(nm), mat(t_), same, A.mult, k=1)
        tt(mat("n" + nm[1]), mat("two"), mat(nm), A.subtract, k=1)
    for nm, e_, c in (("pf0", "e0", 0.0), ("pf1", "e1", 0.0), ("pb0", "e0", 1.0), ("pb1", "e1", 1.0)):
        ts(mat(nm), mat(e_), c, A.is_equal, 2.0, A.mult)
    ts(col("ki", 2), col("ki", 0), 16.0, A.add)
    ts(col("ki", 3), col("ki", 2), 127, A.bitwise_and)
    cp(col("kf", 3), col("ki", 3))
    ts(mat("shf"), mat("mrow"), col("kf", 3), A.is_equal)
    mul(mat("shb"), mat("shf"), -1.0, BOTH)
    mul(mat("idn"), mat("idf"), -1.0, BOTH)
    lin(mat("nq"), mat("mrow"), 32.0, col("kf", 4))
    ts(col("ki", 2), col("ki", 0), 1, A.bitwise_and)
    cp(col("kf", 5), col("ki", 2))
    ts(col("kf", 6), col("kf", 5), 512.0, A.mult)
    ts(col("kf", 8), col("kf", 5), -0.5, A.mult, 0.5, A.add)
    ts(col("kf", 9), ak, 1.0, A.add)
    mul(mat("evn"), mat("idf"), col("kf", 8), BOTH)
    ts(mat("odd"), dm, col("kf", 9), A.is_equal, col("kf", 8), A.mult)

    def umat(p, ub):
        cl, k_ = ("clz", 128) if p == "z" else ("cla", 64)
        for h in (0, 1):
            mms([(bank(ub[h], 0, 512), (T[cl][0:k_, :], (cl, 0, 4), 128), (T.cr[0:k_, 512 * h:512 * h + 512], ("cr", 0, 3 if p == "z" else 1), 512), True, False)])

    def invert(p, vp, ub, sb, lvl1, thr0):
        V, zz, no, jo, jk = "vv" + vp, "zz" + p, v("no" + p, 0, 8), v("jo" + p, 0, 8), 512 * "fbz".index(p)
        for cc in range(8):
            act(v("junk", jk + 64 * cc, jk + 64 * cc + 64), lvl1, F.Sign, bias=col(thr0[0], thr0[1] + cc), scale=-1.0, acc=col("na" + p, cc), extra=0.02)
        ts(no, v("na" + p, 0, 8), 0.5, A.mult, 32.0, A.add)
        tt(v(zz, 0, 128), ind(v("cb" + p, 80, 160), no), mat("cq"), A.is_lt, k=GA)
        cp(v(zz, 128, 256), ind(v("itab", 0, 72), no), k=GA, eng=BOTH)
        for h in (0, 1):
            if p == "z":
                mms([(bank(ub[h], a, 512, 16), v("rep", 128 * a, 128 * a + 128), v("low" + p, 32 * h, 32 * h + 32), False, a == 15) for a in range(16)])
            else:
                both = [("low%s%d" % (p, e), 0, 128) for e in (0, 1)]
                mms([(bank(ub[h], a, 512, 8), v("rep8", 128 * a, 128 * a + 128), v("low" + p, 64 * h, 64 * h + 64, key=both), False, a == 7) for a in range(8)])
        mms([(bank(sb, 0, 128), same, v(zz, 128, 256), True, False), (bank(sb, 0, 128), same, v(zz, 0, 128), False, True)])
        scan(mat("js" + p), mat("seg"), bank(sb, 0, 128), 0.0, A.add, A.min)
        cp(jo, v("js" + p, 15, 128, 16))
        cp(v("jr" + p, 1, 129), bank(sb, 0, 128), eng=BOTH)
        for h in (0, 1):
            scan(v(V, 1 + 512 * h, 513 + 512 * h), bank(ub[h], 0, 512), v("itab", 1 + 512 * h, 513 + 512 * h), col(V, 512 * h), A.max, A.min)
        tt(mat("aa" + p), ind(v(V, 0, 1025), jo), v("jr" + p, 0, 128), A.max, k=GA)

    def hits(x, xo, o, prm, t, split, w=512):
        for e in ((0, 1) if split else (None,)):
            st, d = (1, 0) if e is None else (2, e)
            keys = [[(nm + s_, o, o + w) for s_ in ("01" if e is None else str(e))] for nm in ("ab", "hh")]
            a_ = v("ab", o + d, o + w, st, key=keys[0])
            act(a_, v(x, xo + d, xo + w, st), F.Abs, bias=col(prm, t) if t else col("neg", 2))
            ts(v("hh", o + d, o + w, st, key=keys[1]), a_, col(prm, 7), A.is_le)

    def counts(sb, c0, o):
        for e in (0, 1):
            mms([(bank(sb, c0, c0 + 64), v("sel", 15 - a, 143 - a), v("hh", o + a, o + S, 16, key=("hh%d" % e, o, o + S)), a == 0, a == 15) for a in range(e, 16, 2)])

    def ancestors(p, x, prm, t, lst, ub, sb, o, hc=(0, 512, 1024)):
        for lo, hi in zip(hc, hc[1:]):
            hits(x, lo, o + lo, prm, t, hi == S, hi - lo)
        umat(p, ub)
        counts(sb, 0, o)
        ts(v("w" + p, 0, 64), bank(sb, 0, 64), 2.0, A.max, 383.75, A.add)
        mms([(bank(sb, 128, 194), mat("half"), v("c384", 0, 66), True, False), (bank(sb, 128, 194), mat("half"), v("w" + p, 0, 66), False, True),
             (bank(sb, 200, 264), mat("suf"), v("c384", 0, 64), True, False), (bank(sb, 200, 264), mat("idb"), v("c384", 72, 136), False, False),
             (bank(sb, 200, 264), mat("suf"), v("w" + p, 0, 64), False, True)])
        cs = "cs" + p
        scan(v(cs, 14, 80), v("ones", 0, 66), bank(sb, 128, 194), 0.0, A.mult, A.add)
        add(["dve"], lambda q, e: q.reciprocal(T["rr" + p][:, 0:1], T[cs][:, 78:79]), 0.25, [(cs, 78, 79)], [("rr" + p, 0, 1)])
        r = col("rr" + p, 0)
        tt(v(cs, 80, 144), v(cs, 14, 78), bank(sb, 200, 264), A.subtract, k=1)
        lin(v(cs, 0, 8), v("thr", 0, 8), col(cs, 78), -GAP)
        lin(v("cb" + p, 80, 144), v(cs, 80, 144), r, 128.5)
        lin(v("tt" + p, 0, 64), v("cb" + p, 80, 144), col(cs, 78), col(cs, 79))
        tt(v("rho" + p, 0, 64), v(cs, 80, 144), v("tt" + p, 0, 64), A.subtract)
        mul(v("rr" + p, 2, 4), v("hm", 0, 2), r, BOTH)
        for e in (0, 1):
            lin(v("low" + p, e, 128, 2, key=("low%s%d" % (p, e), 0, 128)), v("rho" + p, 0, 64), col("rr" + p, 2 + e), col("hm", 2 + e))
        invert(p, p, ub, sb, v(cs, 14, 78), (cs, 0))
        cp(mat(lst), mat("aa" + p))

    ancestors("b", "b0s", "par", 0, "lbo0", (4, 5), 6, 0)
    ancestors("f", "f0s", "par", 0, "lfo0", (0, 1), 7, S)
    for t in range(RO):
        last = t == RO - 1
        site[0] = t + 1
        fw, bw, lf, lb = [("f0s", "b0s", "lfo0", "lbo0"), ("fin1", "bo0", "lfi1", "lbo1"), ("fin2", "bo1", "lfi2", "lbo0"), ("fin3", "bin3", "lfi3", "lbi3")][t]
        par, nz_, pi_ = {1: ("parB", "nzB", "piB"), 2: ("parO", "nzO", "piO")}.get(t, ("par", "nzs", "pio"))
        lam, rate = col(par, 4), {"f": col(par, 5), "b": col(par, 6)} if t in (1, 2) else {"f": col("neg", 0), "b": col("neg", 1)}
        bent = A.add if t else A.subtract
        def bend(x, o, bks, l_):
            for h in (0, 1):
                xh, bk = v(x, 512 * h, 512 * h + 512), bank(bks[h], 0, 512)
                act(bk, v(x, 512 * h, 512 * h + 512, key=[xh[1], (l_, 0, 128)]) if l_[2] == "i" else xh, F.Square)
                tt(v("mw", o + 512 * h, o + 512 * h + 512), xh, bk, bent, k=1)
        olds = ((fw, K, lf), (bw, K + S, lb))
        for x, o, l_ in olds:
            if (t, l_[1]) in OPT["early"]:
                bend(x, o, OPT["bb_"] if t else (2, 3), l_)
        for c in range(4):
            cp(v("ba", 512 * c, 512 * c + 512), ind(v(bw, 0, S), v(lb, 32 * c, 32 * c + 32)), k=GA, eng=BOTH)
        for c in range(4):
            cp(v("fi", 512 * c, 512 * c + 512), ind(v(fw, 0, S), v(lf, 32 * c, 32 * c + 32)), k=GA, eng=BOTH)
        umat("z", (4, 5))
        for c in range(4):
            lo, hi = 512 * c, 512 * c + 512
            fi, bk = v("fi", lo, hi), bank(c, 0, 512)
            tt(v("dd", lo, hi), ind(v("ba", 0, K), v(pi_, 32 * c, 32 * c + 32)), fi, A.subtract, k=GA)
            if OPT["padd"][c]:
                mms([(bk, mat("idf"), fi, True, False)], k=4)
                mul(v("tb", lo, hi), v("dd", lo, hi), lam, BOTH)
                mms([(bk, mat("idf"), v("tb", lo, hi), False, True)], k=4)
                hits("bk%d" % c, 0, lo, par, t, c == 3)
                act(v("sm", lo, hi), bk, F.Square)
                tt(v("mw", lo, hi), bk, v("sm", lo, hi), bent, k=1)
            else:
                mul(bk, v("dd", lo, hi), lam, BOTH)
                tt(v("tb", lo, hi), fi, bk, A.add, k=1)
                hits("tb", lo, lo, par, t, c == 3)
                act(bk, v("tb", lo, hi), F.Square)
                tt(v("mw", lo, hi), v("tb", lo, hi), bk, bent, k=1)
            if c % 2:
                counts(6, 64 * (c // 2), S * (c // 2))
        fl = {}
        for p, l_ in (("f", lf), ("b", lb)):
            fl[p] = mat("aa" + p) if l_[2] == "o" else mat("l%sl" % p)
            if l_[2] == "i":
                cp(fl[p], mat(l_))
        mms([(bank(7, 256, 384), mat("evn"), fl["f"], True, False), (bank(7, 256, 384), mat("odd"), fl["b"], False, True)], k=4)
        lin(mat("fcn"), bank(7, 256, 384), 1.0, col("kf", 6))
        for x, o, l_ in olds:
            if (t, l_[1]) not in OPT["early"]:
                bend(x, o, OPT["lb_"][t], l_)
        ts(v("wz", 2, 130), bank(6, 0, 128), 8.5, A.is_ge)
        we, wo, pe_, po_ = v("wz", 2, 130, 2), v("wz", 3, 130, 2), v("wz", 0, 128, 2), v("wz", 1, 128, 2)
        mms([(bank(6, 200, 264), mat("ne"), we, True, False), (bank(6, 200, 264), mat("no"), wo, False, False),
             (bank(6, 200, 264), mat("me"), pe_, False, False), (bank(6, 200, 264), mat("mo"), po_, False, True),
             (bank(6, 128, 192), mat("two"), we, True, False), (bank(6, 128, 192), mat("two"), wo, False, True)])
        for e in OPT["zs"]:
            scan(v("csz", 64 * e, 64 * e + 64), v("ones", 0, 64), bank(6, 128, 192) if e else bank(6, 200, 264), 0.0 if e else -15.5, A.mult, A.add)
        ts(v("ttz", 0, 64), v("csz", 0, 64), 1.5 * 2 ** 28, A.add, 1.5 * 2 ** 28, A.subtract)
        lin(v("cbz", 80, 144), v("csz", 0, 64), 1.0 / 32, 129.0)
        tt(v("lowz", 0, 64), v("csz", 0, 64), v("ttz", 0, 64), A.subtract)
        invert("z", "b", (4, 5), 6, v("csz", 64, 128), ("thr", 8))
        ts(mat("fbk"), mat("nq"), col("csz", 127), A.is_ge)
        tt(mat("fbk"), mat("fbk"), mat("fcn"), A.mult)
        if last:
            for c in range(4):
                x = v("dd", 512 * c, 512 * c + 512)
                if c in OPT["ysq"]:
                    tt(x, x, x, A.mult)
                else:
                    act(x, x, F.Square)
                if c % 2 == 0:
                    act(x, x, F.Exp, scale=-1.0)
                    continue
                y, bk = v("dd", 512 * c - 512, 512 * c), bank(OPT["yb"][c // 2], 0, 512)
                act(bk, x, F.Exp, scale=-1.0)
                tt(y, y, bk, A.add, k=1)
                for j in (2 * c - 2, 2 * c - 1):
                    mms([(bank(7, 0, Z), mat("idf"), v("dd", Z * j, Z * j + Z), j == 0, j == 5)], k=4)
            cp(v("yes", 0, Z), bank(7, 0, Z), eng=BOTH)
            dma("sp", T.ye[:], T.yes[:], 2.2, r=[("yes", 0, Z)])
        first, second = ("f", "b") if t < 2 else ("b", "f")
        for p, sb in ((first, 6), (second, 5 if last else 7)):
            for src in ("fbk", "aaz"):
                mms([(bank(sb, 288, 352), mat("p%s%d" % (p, e)), v(src, e, 128, 2), src == "fbk" and not e, src == "aaz" and e == 1) for e in (0, 1)], k=4)
            cp(v("lo" + p, 0, 64), bank(sb, 288, 352))
        for p, pb in ((first, OPT["pb"][0]), (second, OPT["pb"][1])):
            po = "%so%d" % (p, t % 2)
            sh = p == "b" and not last
            dst = (nxt if p == "b" else prv) if t == 2 else opp if p == first else None
            sc = OPT["scl" if last else "sc"][0 if p == first else 1]
            for h, (lo, hi) in enumerate(zip(sc, sc[1:])):
                hv = ind(v("mw", 0, 2 * K if p == "b" else K + S), v("lo" + p, lo // 16, hi // 16))
                x = v("sq" + p, lo, hi)
                bk = bank(pb[h % len(pb)], 0, hi - lo)
                own = (t, p, h) in OPT["dadd"]
                mms([(bk, mat("shb" if sh else "idb" if last else "idn"), v(nz_, lo, hi), True, own)])
                mul(x, hv, rate[p], BOTH, k=GA)
                if own:
                    tt(x, x, bk, A.add, k=1)
                else:
                    mms([(bk, mat("shf" if sh else "idf"), x, False, True)], k=4)
                ts(v(po, lo, hi), x if own else bk, 0.0 if last else -1.0, A.max, 1.0 if last else 0.0, A.min)
                if last:
                    dma("sp", T["y" + p][:, lo:hi], T[po][:, lo:hi], 2.4, r=[(po, lo, hi)])
                elif dst is not None and hi % 512 == 0:
                    send(dst, v("%sin%d" % (p, t + 1), hi - 512, hi), v(po, hi - 512, hi), "%s%s%d" % (p, "ab"[hi // S], t + 1), tm["tl"] * (1 + hi // S / 3))
            if not last:
                lst = "l%so%d" % (p, (t + 1) % 2)
                ancestors(p, po, {"b": ("parB", "parO", "parF"), "f": ("parF", "par", "parB")}[p][t], t + 1, lst,
                          OPT["ub"][p != first], 6 if p == first else 7, 0 if p == first else S, OPT["hc"][p != first])
                if dst is not None:
                    send(dst, mat("l%si%d" % (p, t + 1)), mat(lst), "%sl%d" % (p, t + 1), tm["ll"])
                if t == 0 and p == second:
                    for to, frm, w_ in (("piO", "pio", 128), ("nzO", "nzs", S)):
                        send(opp, v(to, 0, w_), v(frm, 0, w_, key=[(frm, 0, w_), ("lfi1", 0, 128)]), to, 12.0)
    return ops


def lay(key, eng, loose, dur, rel, ins, outs, free):
    m = len(dur)
    left = [len(y) for y in ins]
    cand = [(key[k], k) for k in range(m) if not left[k]]
    busy = {e: [(0.0, free[e])] for e in QUEUES}
    end = [0.0] * m
    while cand:
        c = min(cand)
        cand.remove(c)
        k = c[1]
        d, got = dur[k], None
        for e in (("act", "dve") if k in loose else (eng[k],)):
            r, u = rel[k][e], 0
            for j, g1, g2 in ins[k]:
                y = end[j] + (g1 if eng[j] == e else g2)
                if y > r:
                    r = y
            if e:
                B = busy[e]
                u = len(B)
                while u and B[u - 1][1] > r:
                    u -= 1
                while u < len(B) and B[u][0] < r + d - 1e-9:
                    if B[u][1] > r:
                        r = B[u][1]
                    u += 1
            if got is None or r < got[0] - 1e-9:
                got = (r, e, u)
        r, e, u = got
        eng[k] = e
        if e:
            busy[e].insert(u, (r, r + d))
        end[k] = r + d
        for j, g1, g2 in outs[k]:
            left[j] -= 1
            if not left[j]:
                cand.append((key[j], j))
    return end


def replay(seq, eng, dur, rel, ins, free):
    fr = dict(free)
    fr[None] = 0.0
    end = [0.0] * len(dur)
    for k in seq:
        e = eng[k]
        r = rel[k][e]
        if e and fr[e] > r:
            r = fr[e]
        for j, g1, g2 in ins[k]:
            y = end[j] + (g1 if eng[j] == e else g2)
            if y > r:
                r = y
        end[k] = fr[e] = r + dur[k]
    return end, fr


def plan(T, topo, core):
    alts = [build(T, topo, core, tm) for tm in SETS]
    ops = alts[0]
    n, sets = len(ops), range(len(SETS))
    dur = [[o["dur"] for o in a] for a in alts]
    lat = [[o["lat"] for o in a] for a in alts]
    ins, outs = [[[] for _ in ops] for s in sets], [[[] for _ in ops] for s in sets]
    for s in sets:
        for i, o in enumerate(ops):
            for j, kd in o["deps"].items():
                g2 = 0.0 if kd == "model" else lat[s][j] + SETS[s]["hop"]
                g1 = 0.0 if ops[j]["kind"] == o["kind"] == "c" and (kd == "order" or o["eng"][0] == "pe") else g2
                ins[s][i].append((j, g1, g2))
                outs[s][j].append((i, g1, g2))
    x = [OPT["seed"]]

    def rnd():
        x[0] = (x[0] * 1103515245 + 12345) % 2147483648
        return x[0] / 2147483648.0

    zero = dict.fromkeys(QUEUES, 0.0)
    none = [dict.fromkeys(o["eng"], 0.0) for o in ops]
    tail = [[dict.fromkeys(o["eng"], lat[s][i]) for i, o in enumerate(ops)] for s in sets]
    on = [o["eng"][0] for o in ops]
    key = [0.0] * n
    for i in range(n - 1, -1, -1):
        key[i] = min([key[j] - g2 for j, g1, g2 in outs[0][i]] + [-lat[0][i]]) - dur[0][i]
    for _ in range(3):
        end = lay(key, on, (), dur[0], none, ins[0], outs[0], zero)
        key = [-y for y in lay([-y for y in end], on, (), dur[0], tail[0], outs[0], ins[0], zero)]
    end = lay(key, on, (), dur[0], none, ins[0], outs[0], zero)
    order = sorted(range(n), key=lambda i: (end[i] - dur[0][i], i))
    other = {"act": "dve", "dve": "act"}
    width, inner = OPT["width"], OPT["inner"]
    for it in range(OPT["tries"]):
        head = [replay(order, on, dur[s], none, ins[s], zero)[0] for s in sets]
        order.sort(key=lambda i: (head[0][i] - dur[0][i], i))
        a = int(rnd() * (n + width / 2) - width / 2)
        a, b = max(a, 0), min(n, a + width)
        W = order[a:b]
        m = len(W)
        loc = {i: k for k, i in enumerate(W)}
        late = set(order[b:])
        rel, out, pin, pout, dw, free, after, base = [], [], [], [], [], [], [], []
        for s in sets:
            q, nx = replay(order[:b - 1:-1] if b < n else [], on, dur[s], tail[s], [[y for y in z if y[0] in late] for z in outs[s]], zero)
            fr = dict(zero)
            for i in order[:a]:
                fr[on[i]] = head[s][i]
            base.append(max([0.0] + [head[s][i] + (g1 if on[i] == on[j] else g2) + q[j] for i in order[:a] for j, g1, g2 in outs[s][i] if j in late]))
            rel.append([{e: max([0.0] + [head[s][j] + (g1 if on[j] == e else g2) for j, g1, g2 in ins[s][i] if j not in loc]) for e in ops[i]["eng"]} for i in W])
            out.append([{e: max([lat[s][i]] + [q[j] + (g1 if on[j] == e else g2) for j, g1, g2 in outs[s][i] if j in late]) for e in ops[i]["eng"]} for i in W])
            pin.append([[(loc[j], g1, g2) for j, g1, g2 in ins[s][i] if j in loc] for i in W])
            pout.append([[(loc[j], g1, g2) for j, g1, g2 in outs[s][i] if j in loc] for i in W])
            dw.append([dur[s][i] for i in W])
            free.append(fr); after.append(nx)
        flex = [k for k, i in enumerate(W) if len(ops[i]["eng"]) > 1]

        def score(seq, eng):
            tot = 0.0
            for s in reversed(sets):
                end, fr = replay(seq, eng, dw[s], rel[s], pin[s], free[s])
                top = max([base[s]] + [y + o[e] for y, o, e in zip(end, out[s], eng)] + [fr[e] + after[s][e] for e in QUEUES])
                tot += SETS[s]["wt"] * (top + 0.01 * sum(end) / m)
            return (tot, seq, eng, [y - d for y, d in zip(end, dw[0])])

        cur = score(list(range(m)), [on[i] for i in W])
        best = (cur[0] + OPT["slack"] * max(0.0, 1 - 1.4 * it / OPT["tries"]) * rnd(),) + cur[1:]
        for step in range(inner):
            eng, key, u = list(cur[2]), list(cur[3]), rnd()
            if u < 0.3 and flex:
                k = flex[int(rnd() * len(flex))]
                eng[k] = other[eng[k]]
                j = flex[int(rnd() * len(flex))]
                if u < 0.1 and eng[j] == eng[k] and j != k:
                    eng[j] = other[eng[j]]
            if u > 0.75:
                i0, d = W[int(rnd() * m)], 4 * (rnd() - 0.5)
                i1 = i0 + 2 + int(rnd() * rnd() * 60)
                key = [y + (d if i0 <= W[k] < i1 else 0.0) for k, y in enumerate(key)]
            elif u > 0.6:
                t0, am = key[int(rnd() * m)], rnd()
                key = [y + (am * rnd() if t0 < y < t0 + 2.0 else 0.0) for y in key]
            elif u > 0.2:
                for _ in range(1 + int(rnd() * 2)):
                    key[int(rnd() * m)] += 3 * (rnd() - 0.5)
            if rnd() < 0.6:
                key = [-y for y in lay([-y - d for y, d in zip(key, dw[0])], eng, (), dw[0], out[0], pout[0], pin[0], after[0])]
            loose = ()
            if rnd() < 0.3:
                t0, sp = cur[3][int(rnd() * m)], 4 * rnd()
                loose = {k for k in flex if t0 <= cur[3][k] < t0 + sp}
            end = lay(key, eng, loose, dw[0], rel[0], pin[0], pout[0], free[0])
            c = score(sorted(range(m), key=lambda k: (end[k] - dw[0][k], W[k])), eng)
            if c[0] <= cur[0] + OPT["temp"] * (1 - it / OPT["tries"]) * (1 - step / inner) * rnd():
                cur = c
                if c[0] < best[0] and 3 * step > inner:
                    best = c
        order[a:b] = [W[k] for k in best[1]]
        for k, i in enumerate(W):
            on[i] = best[2][k]
    ends = [replay(order, on, dur[s], none, ins[s], zero)[0] for s in sets]
    return order, on, [[y + z for y, z in zip(ends[s], lat[s])] for s in sets]


PLAN = []


def rank_program(g, core, T, topo):
    if T.rank_of(core) is None:
        return
    if not PLAN:
        PLAN.extend(plan(T, topo, core))
    order, on, done = PLAN
    ops = build(T, topo, core, SETS[0])
    Q = {"pe": g.tensor, "dve": g.vector, "act": g.scalar, "pool": g, "sp": g.sync}

    def waits(i):
        o = ops[i]
        return [j for j, kd in o["deps"].items()
                if kd != "model" and not (ops[j]["kind"] == o["kind"] == "c" and on[j] == on[i] and (kd == "order" or on[i] == "pe"))]

    pos = {}
    seen = {e: 0 for e in Q}
    for i in order:
        if ops[i]["kind"] == "c":
            seen[on[i]] += 1
            pos[i] = seen[on[i]]
    know = {e: {} for e in Q}
    after = {}
    need = {}
    signal = set()
    for i in order:
        o = ops[i]
        if o["kind"] == "arr":
            after[i] = {o["sem"]: 1}
            continue
        kn = know[on[i]]
        lst = []
        for j in sorted(waits(i), key=lambda j: -done[0][j]):
            d = ops[j]
            key, val = (on[j], pos[j]) if d["kind"] == "c" else (d["sem"], 1)
            if kn.get(key, 0) >= val:
                continue
            lst.append(j)
            signal.add(j)
            for k_, x in after[j].items():
                if kn.get(k_, 0) < x:
                    kn[k_] = x
        need[i] = lst
        a = dict(kn)
        if o["kind"] == "c":
            a[on[i]] = pos[i]
        else:
            a[o["sem"]] = 1
        after[i] = a
    count = {e: 0 for e in Q}
    val = {}
    for i in order:
        o = ops[i]
        if o["kind"] == "arr":
            continue
        e = on[i]
        for j in need[i]:
            d = ops[j]
            if d["kind"] == "c":
                Q[e].wait_ge(T.sem[on[j]], val[j])
            else:
                Q[e].wait_ge(T.sem[d["sem"]], d["cnt"])
        ins = o["fn"](Q[e], e)
        if o["kind"] == "c":
            if i in signal:
                count[e] += 1
                val[i] = count[e]
                ins.then_inc(T.sem[e], 1)
        elif o["kind"] == "dma":
            ins.then_inc(T.sem[o["sem"]], 16)
    for o in ops:
        if o["kind"] != "c":
            g.wait_ge(T.sem[o["sem"]], o["cnt"])
    for e in ("pe", "dve", "act", "pool"):
        if count[e]:
            g.wait_ge(T.sem[e], count[e])
